import numpy as np, ml_dtypes
CORES = [13,21,141,149]
N = 4
BF = ml_dtypes.bfloat16
A, W, B, BL, RO = 384, 4096, 32, 3, 4
def parts(rng):
    share = rng.choice(np.array([0.5, 0.75, 0.95]), (N, 8, 1, 1)) * rng.random((N, 8, 1, A))
    s = np.where(rng.random((N, 8, 16, A)) < share, 4096, rng.integers(0, 4096, (N, 8, 16, A)))
    l = np.minimum(np.maximum(rng.integers(90, 201, (N, 8, 1, A)) + rng.integers(-60, 61, (N, 8, 16, A)), 0), 255)
    return s, l, rng.integers(0, 4096, (N, 8, A)), rng.integers(0, 256, (N, 8, 16, W))
def pack(s, l, k, f):
    return {"sr": np.ascontiguousarray(s.reshape(N, 128, A)).astype(np.int32), "lim": np.ascontiguousarray(l.reshape(N, 128, A)).astype(np.int32),
            "u": np.ascontiguousarray(k).astype(np.int32), "fit": np.ascontiguousarray(f.reshape(N, 128, W)).astype(np.float32).astype(BF)}
def setup_inputs(rng):
    return pack(*parts(rng))
def setup_inputs_ties(rng):
    s, l, k, f = parts(rng); g = rng.permutation(8); cnt = rng.integers(0, 17, (N, 8, A))
    cnt[:, g[0]] = rng.integers(15, 17, (N, A)); cnt[:, g[1]] = rng.choice(np.array([0, 15, 16]), (N, A)); cnt[:, g[2]] = 8
    cnt[:, g[3]] = 0; cnt[:, g[4]] = 16; cnt[:, g[4], 0] = 0; cnt[:, g[4], A - 1] = 0
    cnt[:, g[5]] = 0
    for q in rng.permutation(N)[1:]: cnt[q, g[5], rng.permutation(A // 2)[:A // 32]] = 1
    l[:, g[[0, 1, 2, 5]]] = 255
    whole = rng.integers(0, 4096, s.shape)
    s = np.where(np.argsort(rng.random(s.shape), axis=2) < cnt[:, :, None, :], 4096, whole)
    return pack(s, l, k, f)
def setup_inputs_level(rng):
    s, l, k, f = parts(rng); base = rng.integers(1, 255, (1, 8, 16, 1))
    n = rng.choice(np.array([0, 3, 5, 7, 7, 8, 8, 11, 11, 12]), (N, 8, 1, W))
    over = np.argsort(rng.random(f.shape, dtype=np.float32), axis=2) < n
    f = base + np.where(over, 1, -rng.integers(0, 2, f.shape))
    return pack(s, l * 0 + base, k, f)
def setup_inputs_ends(rng):
    s, l, k, f = parts(rng); g = rng.permutation(8)
    e = rng.choice(np.array([0, 1, 31, 32, 2048, 4094, 4095]), s.shape)
    s = np.where((s < 4096) & (rng.random((N, 8, 1, A)) < 0.7), e, s)
    k = np.where(rng.random(k.shape) < 0.7, rng.choice(np.array([0, 1, 31, 32, 2048, 4094, 4095, 3099, 2102, 1105]), k.shape), k)
    m = rng.integers(0, 6, (N, 8, 1, A))
    l = np.where(m == 0, 0, np.where(m == 1, 255, np.where(m == 2, 255 * rng.integers(0, 2, l.shape), l)))
    f[:, g[:4]] = 255 * rng.integers(0, 2, (N, 4, 16, W))
    f[:, :, :, 0] = 255 * rng.integers(0, 2, (N, 8, 16)); f[:, :, :, W - 1] = 255 * rng.integers(0, 2, (N, 8, 16))
    q = int(rng.integers(0, N)); hole = (np.argsort(rng.random((8, 16, 1)), axis=1) < 8) == (np.arange(A) < A // 2)
    s[q] = np.where(hole, 4096, np.where(rng.random(hole.shape) < 0.7, e[q], rng.integers(0, 4096, hole.shape))); l[q] = 255
    return pack(s, l, k, f)
def setup_inputs_alike(rng):
    s, l, k, f = parts(rng); o = rng.permutation(8); g = o[:4]; d = int(o[4]); q = rng.permutation(N)
    s[q[0]] = rng.integers(0, 4096, (8, 16, A)); s[q[1]] = np.where(rng.random((8, 16, A)) < 0.9, 4096, rng.integers(0, 4096, (8, 16, A)))
    for h in g:
        few = rng.integers(0, 4096, 5); s[:, h] = np.where(s[:, h] < 4096, few[rng.integers(0, 5, (N, 16, A))], 4096)
        k[:, h] = int(rng.integers(0, 4096))
    f[:, d] = f[:, d] % 101; f[q[0], d] = rng.integers(200, 256, (16, W)); l[q[0], d] = rng.integers(100, 200, (16, A))
    return pack(s, l, k, f)
def setup_inputs_spread(rng):
    s, l, k, f = parts(rng)
    s = np.where(s < 4096, np.minimum(np.exp2(12 * rng.random(s.shape)).astype(np.int64), 4095), 4096)
    k = np.minimum(np.exp2(12 * rng.random(k.shape)).astype(np.int64), 4095)
    l = np.minimum((np.exp2(4 + 4 * rng.random((N, 8, 1, A))) * (0.5 + 0.5 * rng.random(l.shape))).astype(np.int64), 255)
    f = np.minimum((np.exp2(8 * rng.random((N, 8, 1, W))) * rng.random(f.shape)).astype(np.int64), 255)
    return pack(s, l, k, f)
def check_inputs(d):
    bad = []
    for n, hi in (("sr", 4096), ("lim", 255), ("u", 4095), ("fit", 255)):
        a = np.asarray(d[n]).astype(np.float64)
        if not (np.min(a) >= 0 and np.max(a) <= hi): bad.append("range of " + n)
    a = np.asarray(d["fit"]).astype(np.float32)
    if not np.all(a == np.floor(a)): bad.append("whole numbers in fit")
    return bad
def records(f, s, v):
    c = ((s * v[:, :, None, :]) >> 5) & (W - 1)
    return np.take_along_axis(f, c.reshape(N, 8, 1, -1), 3).reshape(N, 8, 16, 16, -1)
def reference(sr, lim, u, fit):
    s = sr.astype(np.int64).reshape(N, 8, 16, A); l = lim.astype(np.int16).reshape(N, 8, 16, A); k = u.astype(np.int64)
    f = fit.astype(np.float32).astype(np.int16).reshape(N, 8, 16, W); h = A // 2
    for t in range(RO):
        over = np.sum(records(f, s, (k + 997 * t) & 4095) > l[:, :, :, None, :], axis=2)
        s = np.where(over >= 12, 4096, s)
        holes = np.minimum(np.sum(s == 4096, axis=2), 15)
        o = np.argsort(holes, axis=2, kind="stable")
        s = np.take_along_axis(s, o[:, :, None, :], 3); l = np.take_along_axis(l, o[:, :, None, :], 3); k = np.take_along_axis(k, o, 2)
        have = s[..., :h]; give = s[..., h:][..., ::-1]
        good = np.sum(records(f, give, (k[..., :h] + 997 * t) & 4095) <= l[:, :, :, None, :h], axis=2)
        move = (have == 4096) & (give < 4096) & (good >= 9)
        s = np.concatenate([np.where(move, give, have), np.where(move, 4096, give)[..., ::-1]], axis=3)
        for b in range(BL):
            c = slice(A - BL * B + b * B, A - BL * B + (b + 1) * B)
            s[..., c] = np.roll(s[..., c], b + 1, axis=0); l[..., c] = np.roll(l[..., c], b + 1, axis=0); k[..., c] = np.roll(k[..., c], b + 1, axis=0)
    return {"ysr": s.reshape(N, 128, A).astype(np.float32), "ylim": l.reshape(N, 128, A).astype(np.float32), "yu": k.astype(np.float32)}

@@ -1,0 +1,617 @@
+from concourse.bass import DstId, RemoteDMATransfer
+from concourse.mybir import AluOpType, ActivationFunctionType
+
+ALU = AluOpType
+AF = ActivationFunctionType
+A, H, ST, BK, NB, RO, W = 384, 192, 288, 32, 3, 4, 4096
+HOLE = 4096.0
+BIG = 131072.0
+CFG = {"gam": 1.3, "sig": 3.2, "cyc": 0.83, "pe": 0.42, "hop": 80, "vfix": 20, "afix": 60, "riss": 800, "rlat": 2000}
+
+
+def sb(n, dtype):
+    return ("sbuf", [128, n], dtype)
+
+
+SCRATCH = {
+    "FIT": sb(W, "bfloat16"), "SRI": sb(A, "int32"), "LMI": sb(A, "int32"), "UI": sb(A, "int32"), "UF": sb(A, "float32"),
+    "XI": sb(144, "float32"), "XG": sb(128, "float32"), "XT": sb(4, "float32"), "PI": sb(8, "int32"),
+    "COL": sb(16, "float32"), "NUM": sb(A, "bfloat16"), "ID": sb(128, "bfloat16"), "NI": sb(128, "bfloat16"),
+    "Z": sb(144, "bfloat16"), "BB": sb(128, "bfloat16"), "SV": sb(512, "bfloat16"), "R8": sb(128, "float32"),
+    "CKD": sb(128, "bfloat16"), "CKA": sb(64, "bfloat16"), "SW": sb(A, "float32"), "SS": sb(A, "float32"),
+    "LIM0": sb(A, "bfloat16"), "LIM1": sb(A, "bfloat16"), "KV0": sb(A, "bfloat16"), "KV1": sb(A, "bfloat16"),
+    "PR": sb(A, "int32"), "CX": sb(A, "int32"), "CU": sb(A, "uint16"), "KA": sb(A, "int32"), "KB": sb(A, "int32"),
+    "LX": sb(16 * 256, "bfloat16"), "L4": sb(4 * 256, "bfloat16"),
+    "IND": sb(16 * A, "bfloat16"), "REC": sb(16 * A, "bfloat16"),
+    "HS": sb(A, "bfloat16"), "JK": sb(A, "bfloat16"), "E": sb(A, "bfloat16"), "M": sb(A, "bfloat16"),
+    "OW": sb(A, "bfloat16"), "BASE": sb(4, "float32"), "PL": sb(24, "uint16"), "OL": sb(24, "uint16"),
+    "TM": sb(H, "bfloat16"),
+    "M1": ("sbuf", [128, RO * NB, 3 * BK], "float32"), "L1": ("sbuf", [128, RO * NB, 3 * BK], "float32"),
+    "M2": sb(RO * NB * BK, "float32"), "L2": sb(RO * NB * BK, "float32"),
+    "OUTL": sb(ST, "float32"), "OUTK": sb(A, "float32"),
+}
+for bank_ in ("D0", "D1", "PA", "PB", "PC", "V", "H1", "H2"):
+    SCRATCH[bank_] = ("psum", [128, 512], "float32")
+NDMA = 12
+SEMAPHORES = (["q_v", "q_a", "q_p", "q_g", "sent"] + ["dm%d" % k for k in range(NDMA)]
+              + ["a1_%d" % t for t in range(RO)] + ["a2_%d" % t for t in range(RO)])
+
+
+def routes(T, topo):
+    n = len(T.cores)
+    out = {}
+    for r, src in enumerate(T.cores):
+        used = []
+        for b in range(NB):
+            dst = T.cores[(r + 1 + b) % n]
+            via = None
+            if not topo.may_write(src, dst):
+                can = [c for c in topo.cores_of(src)
+                       if c not in T.cores and c not in used and topo.may_write(c, dst)]
+                can.sort(key=lambda c: topo.die(c) != topo.die(src))
+                via = can[0]
+                used.append(via)
+            out[(r, b)] = (dst, via)
+    return out
+
+
+def bits(engines):
+    m = 0
+    for e in engines:
+        m |= 1 << e
+    return m
+
+
+def relay_masks(T, topo, rt, r):
+    src = T.cores[r]
+    bl = [b for b in range(NB) if rt[(r, b)][1] is not None]
+    out = {}
+    for j, b in enumerate(bl):
+        eng = topo.engines(src, rt[(r, b)][1])
+        n = len(eng) // len(bl)
+        out[b] = eng[j * n:(j + 1) * n]
+    return out
+
+
+def piece(T, kind, land, t, b):
+    if kind == 1:
+        lo = BK if t == RO - 1 else 0
+        return T["L1" if land else "M1"][:, NB * t + b, lo:3 * BK]
+    c = (NB * t + b) * BK
+    return T["L2" if land else "M2"][:, c:c + BK]
+
+
+def relay_program(g, core, T, topo, rt):
+    mine = [k for k in rt if rt[k][1] == core]
+    total = 0
+    for (r, b) in mine:
+        dst = rt[(r, b)][0]
+        n_in = len(relay_masks(T, topo, rt, r)[b])
+        rid, pid = topo.addr(dst, core)
+        for t in range(RO):
+            for kind in (1, 2):
+                sem = T.sem["a%d_%d" % (kind, t)]
+                g.wait_ge(sem, n_in)
+                ap = piece(T, kind, True, t, b)
+                g.remote_dma(ap, ap, sem, T.sem.sent, pid, rid, topo.mask(core, dst))
+                total += len(topo.engines(core, dst))
+    if total:
+        g.wait_ge(T.sem.sent, total)
+
+
+def clash(x, y, qx, qy):
+    if SCRATCH[x[0]][0] == "psum":
+        if qx == "p" and qy == "p":
+            return False
+        if qx != qy:
+            return True
+    return (x[3] or y[3]) and x[1] < y[2] and y[1] < x[2]
+
+
+def arrange(nodes):
+    n = len(nodes)
+    pred = [dict() for _ in nodes]
+    by_buf = {}
+    for k, nd in enumerate(nodes):
+        acc = set(x for o in nd["ops"] for x in o["acc"])
+        for x in acc:
+            for (j, y) in by_buf.get(x[0], []):
+                if j in pred[k]:
+                    continue
+                if nd["q"] == "p" and nodes[j]["q"] == "p":
+                    if SCRATCH[x[0]][0] == "psum":
+                        pred[k][j] = 0
+                elif clash(x, y, nd["q"], nodes[j]["q"]):
+                    pred[k][j] = nodes[j]["lat"] + CFG["hop"]
+        for j, d in nd["after"]:
+            pred[k][j] = max(pred[k].get(j, 0), d)
+        for x in acc:
+            by_buf.setdefault(x[0], []).append((k, x))
+    succ = [[] for _ in nodes]
+    for k in range(n):
+        for j in pred[k]:
+            succ[j].append(k)
+    level = [0.0] * n
+    for k in range(n - 1, -1, -1):
+        level[k] = nodes[k]["busy"] + 0.001 + max([nodes[k]["lat"]] + [pred[s][k] + level[s] for s in succ[k]])
+    taken = {}
+    for k in sorted(range(n), key=lambda j: -level[j]):
+        nd = nodes[k]
+        start = max([0.0] + [nodes[j]["end"] + d for j, d in pred[k].items()])
+        if nd["q"]:
+            spans = taken.setdefault(nd["q"], [])
+            for lo, hi in spans:
+                if start + nd["busy"] <= lo:
+                    break
+                start = max(start, hi)
+            spans.append((start, start + nd["busy"]))
+            spans.sort()
+        nd["start"], nd["end"] = start, start + nd["busy"]
+    return [o for k in sorted(range(n), key=lambda j: (nodes[j]["start"], j)) for o in nodes[k]["ops"]]
+
+
+def emit(g, T, ops):
+    eng = {"v": g.vector, "a": g.scalar, "p": g.tensor, "g": g, "s": g.sync}
+    known = {q: {} for q in eng}
+    seq = {q: 0 for q in eng}
+    by_buf = {}
+    for k, op in enumerate(ops):
+        q = op["q"]
+        if q is not None and op.get("sem") is None:
+            seq[q] += 1
+            op["line"], op["pos"] = q, seq[q]
+        else:
+            op["line"], op["pos"] = "x%d" % k, 1
+        op["waits"] = []
+        op["marked"] = False
+        op["knows"] = {}
+        if q is not None:
+            need = {}
+            for x in op["acc"]:
+                for (j, y) in by_buf.get(x[0], []):
+                    o = ops[j]
+                    oq = o["line"]
+                    if known[q].get(oq, 0) < o["pos"] and clash(x, y, op["line"], oq) and need.get(oq, (0, 0))[0] < o["pos"]:
+                        need[oq] = (o["pos"], j)
+            for (pos, j) in sorted(need.values(), key=lambda z: -z[1]):
+                o = ops[j]
+                if known[q].get(o["line"], 0) >= o["pos"]:
+                    continue
+                op["waits"].append(j)
+                o["marked"] = True
+                for ln, p in o["knows"].items():
+                    if known[q].get(ln, 0) < p:
+                        known[q][ln] = p
+            op["knows"] = dict(known[q])
+        op["knows"][op["line"]] = op["pos"]
+        for x in op["acc"]:
+            by_buf.setdefault(x[0], []).append((k, x))
+    count = {q: 0 for q in eng}
+    ends = {}
+    for op in ops:
+        q = op["q"]
+        for j in op["waits"]:
+            eng[q].wait_ge(T.sem[ops[j]["sem"]], ops[j]["val"])
+        if q is None:
+            ends[op["sem"]] = op["val"]
+            continue
+        ins = op["fn"]()
+        if op.get("remote"):
+            continue
+        if op.get("sem") is not None:
+            ins.then_inc(T.sem[op["sem"]], 16)
+            ends[op["sem"]] = op["val"]
+        elif op["marked"]:
+            count[q] += 1
+            op["sem"], op["val"] = "q_" + q, count[q]
+            ins.then_inc(T.sem[op["sem"]], 1)
+            ends[op["sem"]] = count[q]
+    return ends
+
+
+def rank_program(g, core, T, topo):
+    rt = routes(T, topo)
+    rank = T.rank_of(core)
+    if rank is None:
+        relay_program(g, core, T, topo, rt)
+        return
+    nodes = []
+    ndma = [0]
+    sent = [0]
+    V, S, P = g.vector, g.scalar, g.tensor
+    cyc = CFG["cyc"]
+
+    def at(ap, n, *regions):
+        return (ap, n, (SCRATCH[regions[0][0]][0], SCRATCH[regions[0][0]][2] in ("bfloat16", "uint16"))) + regions
+
+    def c(name, lo, hi, step=1):
+        ap = T[name][:, lo:hi:step] if step != 1 else T[name][:, lo:hi]
+        return at(ap, len(range(lo, hi, step)), (name, lo, hi))
+
+    def rev(name, lo, hi):
+        return at(T[name][:, hi - 1:lo - 1:-1] if lo > 0 else T[name][:, hi - 1::-1], hi - lo, (name, lo, hi))
+
+    def win(name, n, off, lo, hi):
+        return (T[name][:, 0:n].indirect(T[off][:, lo:hi]), 16 * (hi - lo), "win", (name, 0, n), (off, lo, hi))
+
+    def op(q, fn, outs, ins, busy, lat=0.0, join=False, after=(), **kw):
+        acc = []
+        for o in outs:
+            if o[2] == "win":
+                acc += [o[3] + (True,), o[4] + (False,)]
+            else:
+                acc += [r + (True,) for r in o[3:]]
+        for i in ins:
+            if isinstance(i, tuple):
+                acc += [r + (False,) for r in i[3:]]
+        d = {"q": q, "fn": fn, "acc": acc}
+        d.update(kw)
+        if join:
+            nodes[-1]["ops"].append(d)
+            nodes[-1]["busy"] += busy
+        else:
+            nodes.append({"q": q, "ops": [d], "busy": busy, "lat": lat, "after": list(after)})
+        return len(nodes) - 1
+
+    def val(x):
+        return x[0] if isinstance(x, tuple) else x
+
+    def vcost(out, in0, per=None):
+        if out[2] == "win":
+            return 50 + out[1] * CFG["sig"]
+        if in0[2] == "win":
+            return 50 + out[1] * CFG["gam"]
+        if per is None:
+            per = 0.5 if out[2][1] and in0[2][1] else 1.0
+        return CFG["vfix"] + max(64, out[1] * per) * cyc
+
+    def ts(out, in0, s1, op0, s2=None, op1=None):
+        if op1 is None:
+            op("v", lambda: V.tensor_scalar(out[0], in0[0], val(s1), None, op0), [out], [in0, s1], vcost(out, in0))
+        else:
+            op("v", lambda: V.tensor_scalar(out[0], in0[0], val(s1), val(s2), op0, op1), [out], [in0, s1, s2], vcost(out, in0))
+
+    def tt(out, in0, in1, o):
+        op("v", lambda: V.tensor_tensor(out[0], in0[0], in1[0], o), [out], [in0, in1], vcost(out, in0, 1.0))
+
+    def cp(out, in_):
+        op("v", lambda: V.tensor_copy(out[0], in_[0]), [out], [in_], vcost(out, in_))
+
+    def act(out, in_, func=AF.Identity, bias=0.0, scale=1.0, accum=None):
+        busy = 65 + out[1] * CFG["gam"] if in_[2] == "win" else CFG["afix"] + out[1] * cyc
+        if accum is None:
+            op("a", lambda: S.activation(out[0], in_[0], func, bias=val(bias), scale=val(scale)),
+               [out], [in_, bias, scale], busy)
+        else:
+            op("a", lambda: S.activation(out[0], in_[0], func, bias=val(bias), scale=val(scale), accum_out=accum[0]),
+               [out, accum], [in_, bias, scale], busy)
+
+    def mm(out, lhsT, rhs, start=True, stop=True, join=False):
+        op("p", lambda: P.matmul(out[0], lhsT[0], rhs[0], start, stop), [out], [lhsT, rhs],
+           max(64, rhs[1]) * CFG["pe"] * (1 if rhs[2][1] else 4), join=join)
+
+    def dma(q, out, in_, lat, after=()):
+        e = g.sync if q == "s" else g.scalar
+        name = "dm%d" % ndma[0]
+        ndma[0] += 1
+        return op(q, lambda: e.dma_start(out[0], in_[0]), [out], [in_], 60, lat, after=after, sem=name, val=16)
+
+    def hbm(ap):
+        return (ap, 0, "hbm")
+
+    def iota(out, pattern, base, cm, small):
+        busy = 130 + 2 * out[1] * cyc
+        if small:
+            op("g", lambda: g.iota(out[0], pattern, base, cm, allow_small_or_imprecise_dtypes=True), [out], [], busy)
+        else:
+            op("g", lambda: g.iota(out[0], pattern, base, cm), [out], [], busy)
+
+    def col(k):
+        return c("COL", k, k + 1)
+
+    def region(kd, land, t, b):
+        if kd == 1:
+            return at(None, 0, ("L1" if land else "M1", NB * t + b, NB * t + b + 1))
+        return at(None, 0, ("L2" if land else "M2", (NB * t + b) * BK, (NB * t + b + 1) * BK))
+
+    rm = relay_masks(T, topo, rt, rank)
+    chain = []
+
+    def send(kd, t):
+        sem = T.sem["a%d_%d" % (kd, t)]
+        trs = []
+        edges = []
+        for b in rm:
+            rid, pid = topo.addr(rt[(rank, b)][1], core)
+            trs.append(RemoteDMATransfer(dst_ids=[DstId(rid=rid, pnc=pid)], dma_engine_mask=bits(rm[b]),
+                                         remote_sem=sem, src=piece(T, kd, False, t, b), dst=piece(T, kd, True, t, b)))
+            sent[0] += len(rm[b])
+        if trs:
+            k = op("g", lambda: g.remote_dma_fused(trs, local_sem=T.sem.sent), [],
+                   [region(kd, False, t, b) for b in rm], CFG["riss"], after=chain[-1:], remote=True)
+            chain.append((k, 0))
+            edges.append((k, 2 * CFG["rlat"] + CFG["riss"] + 2 * CFG["hop"]))
+        for b in range(NB):
+            if b in rm:
+                continue
+            dst = rt[(rank, b)][0]
+            rid, pid = topo.addr(dst, core)
+            sent[0] += len(topo.engines(core, dst))
+            k = op("g", lambda b=b, dst=dst, rid=rid, pid=pid: g.remote_dma(
+                piece(T, kd, True, t, b), piece(T, kd, False, t, b), sem, T.sem.sent, pid, rid,
+                topo.mask(core, dst)), [], [region(kd, False, t, b)], CFG["riss"], remote=True)
+            edges.append((k, CFG["rlat"]))
+        n = 0
+        for (r, b), (dst, via) in rt.items():
+            if dst == core:
+                n += len(topo.engines(via if via is not None else T.cores[r], core))
+        op(None, None, [region(kd, True, t, b) for b in range(NB)], [], 0, after=edges,
+           sem="a%d_%d" % (kd, t), val=n)
+
+    def landed(t, part):
+        return at(T.L1[:, NB * t:NB * (t + 1), part * BK:(part + 1) * BK], NB * BK, ("L1", NB * t, NB * (t + 1)))
+
+    def m1(t, b, part):
+        k = NB * t + b
+        return at(T.M1[:, k, part * BK:(part + 1) * BK], BK, ("M1", k + part / 4.0, k + (part + 1) / 4.0))
+
+    ID, NI, BB = c("ID", 0, 128), c("NI", 0, 128), c("BB", 0, 128)
+
+    def sel(r):
+        return c("Z", 15 - r, 143 - r)
+
+    def sv(t):
+        return c("SV", 128 * t, 128 * (t + 1))
+
+    def spread(lim, lo, hi, on=None):
+        for i in range(16):
+            (on or cp)(at(T.LX[:, 16 * lo + i:16 * hi:16], hi - lo, ("LX", 16 * lo + i / 32.0, 16 * lo + (i + 1) / 32.0)),
+                       c(lim, lo, hi))
+
+    def spread4(lim, lo, hi):
+        for j in range(4):
+            cp(at(T.L4[:, 4 * lo + j:4 * hi:4], hi - lo, ("L4", 4 * lo + j / 8.0, 4 * lo + (j + 1) / 8.0)), c(lim, lo, hi))
+        for j in range(4):
+            cp(at(T.LX[:, 16 * lo + j:16 * hi:4], 4 * (hi - lo), ("LX", 16 * lo + j / 32.0, 16 * lo + (j + 1) / 32.0)),
+               at(T.L4[:, 4 * lo:4 * hi], 4 * (hi - lo), ("L4", 4 * lo, 4 * lo + 1)))
+
+    def idx1(lo, hi, s):
+        tt(c("PR", lo, hi), s, c("V", lo, hi), ALU.mult)
+
+    def idx2(lo, hi):
+        ts(c("CX", lo, hi), c("PR", lo, hi), 5, ALU.arith_shift_right, W - 1, ALU.bitwise_and)
+        cp(c("CU", lo, hi), c("CX", lo, hi))
+
+    def by_vector(lo, hi, part, bank, term=None):
+        lx = at(T.LX[:, 16 * lo:16 * hi], 16 * (hi - lo), ("LX", 16 * part, 16 * part + 1))
+        tt(c("IND", 16 * lo, 16 * hi), win("FIT", W, "CU", lo, hi), lx, ALU.is_gt)
+        mm(c(bank, lo, hi), ID, term or c("CKD", 0, hi - lo), True, False)
+        for i in range(16):
+            mm(c(bank, lo, hi), sel(i), c("IND", 16 * lo + i, 16 * hi, 16), False, i == 15, join=i != 0)
+
+    def by_scalar(lo, hi, lim, bank, term=None, one="D0"):
+        n = hi - lo
+        parts = [("D0", 0, 8), ("D1", 8, 16)] if n > 32 else [(one, 0, 16)]
+        act(c("REC", 16 * lo, 16 * hi), win("FIT", W, "CU", lo, hi))
+        for d, i0, i1 in parts:
+            for i in range(i0, i1):
+                mm(c(d, (i - i0) * n, (i - i0 + 1) * n), NI, c(lim, lo, hi), i == i0, False, join=i != i0)
+            for i in range(i0, i1):
+                mm(c(d, (i - i0) * n, (i - i0 + 1) * n), ID, c("REC", 16 * lo + i, 16 * hi, 16), False, i == i1 - 1,
+                   join=i != i0)
+            act(c("IND", 16 * lo + i0 * n, 16 * lo + i1 * n), c(d, 0, (i1 - i0) * n), AF.Sign, bias=-0.5)
+        mm(c(bank, lo, hi), ID, term or c("CKA", 0, n), True, False)
+        for d, i0, i1 in parts:
+            for i in range(i0, i1):
+                mm(c(bank, lo, hi), sel(i), c("IND", 16 * lo + i * n, 16 * lo + (i + 1) * n), False, i == 15, join=i != i0)
+
+    def drop(lo, hi, s, bank):
+        tt(c("SW", lo, hi), s, c(bank, lo, hi), ALU.max)
+
+    def tally(lo, hi):
+        act(c("HS", lo, hi), c("SW", lo, hi), AF.Sign, bias=-(HOLE - 0.5))
+        mm(c("H2", lo, hi), BB, c("HS", lo, hi))
+        mm(c("H1", lo, hi), BB, c("HS", lo, hi))
+
+    def wrap(src, bank):
+        for r in range(16):
+            mm(c(bank, 0, 24), sel(r), c(src, r, A, 16), r == 0, r == 15, join=r != 0)
+
+    def order():
+        ts(c("E", 0, A), c("H1", 0, A), 14.0, ALU.min, col(0), ALU.is_equal)
+        act(c("JK", 0, A), c("H2", 0, A), AF.Sign, bias=col(1), scale=-1.0, accum=c("BASE", 0, 1))
+        e, st = c("E", 0, A), c("D0", 0, A)
+        op("v", lambda: V.tensor_tensor_scan(st[0], e[0], e[0], T.BASE[:, 0:1], ALU.add, ALU.add),
+           [st], [e, c("BASE", 0, 1)], vcost(st, e))
+        tt(c("M", 0, A), e, st, ALU.mult)
+        wrap("M", "D1")
+        ts(c("PL", 0, 24), c("D1", 0, 24), 1.0 / 8192, ALU.mult, float(H - 1), ALU.add)
+        cp(win("OW", A, "PL", 0, 24), c("NUM", 0, A))
+        wrap("OW", "D1")
+        ts(c("OL", 0, 24), c("D1", 0, 24), 1.0 / 65536, ALU.mult, float(H), ALU.add)
+
+    def pick(src, lo, hi):
+        return win(src, A, "OL", lo // 16, hi // 16)
+
+    def sort_s(lo, hi):
+        ts(c("SS", lo, hi), pick("SW", lo, hi), HOLE, ALU.min)
+
+    def term_v(lo, hi):
+        act(c("TM", lo, hi), c("SS", lo, hi), bias=BIG * HOLE - 7 * HOLE, scale=-BIG)
+
+    def term_a(lo, hi):
+        act(c("TM", lo, hi), c("SS", lo, hi), bias=BIG * HOLE + HOLE, scale=-BIG)
+
+    def rob(lo, hi, bank, give_out):
+        ts(c("H2", lo, hi), c(bank, lo, hi), 0.5, ALU.is_le, HOLE, ALU.mult)
+        tt(c("H1", lo, hi), rev("SS", A - hi, A - lo), c(bank, lo, hi), ALU.max)
+        tt(give_out, rev("SS", A - hi, A - lo), c("H2", lo, hi), ALU.max)
+        tt(c("SS", lo, hi), c("SS", lo, hi), c("H1", lo, hi), ALU.min)
+
+    dma("a", at(T.UI[0:8, :], A, ("UI", 0, A)), hbm(T.u[:]), 1900)
+    k = dma("s", c("SRI", 0, A), hbm(T.sr[:]), 2600)
+    k = dma("s", c("LMI", 0, A), hbm(T.lim[:]), 3300, [(k, 0)])
+    dma("s", c("FIT", 0, W), hbm(T.fit[:]), 7400, [(k, 0)])
+    iota(c("PI", 0, 1), [[0, 1]], 0, 1, False)
+    iota(col(2), [[0, 1]], 0, 1, True)
+    iota(c("XG", 0, 128), [[1, 8], [0, 16]], 0, 0, True)
+    iota(c("XI", 0, 144), [[1, 144]], 0, 0, True)
+    iota(c("XT", 0, 4), [[1, 4]], 0, 0, True)
+    iota(c("NUM", 0, A), [[1, A]], -H, 0, True)
+    op("v", lambda: V.memset(T.CKD[:], -11 * HOLE), [c("CKD", 0, 128)], [], 70)
+    op("v", lambda: V.memset(T.CKA[:], -7 * HOLE), [c("CKA", 0, 64)], [], 70)
+    pi = c("PI", 0, 1)
+    ts(c("PI", 1, 2), pi, 15, ALU.bitwise_and)
+    ts(c("PI", 2, 3), pi, 4, ALU.arith_shift_right)
+    ts(c("PI", 3, 4), pi, 1, ALU.arith_shift_right, 7, ALU.bitwise_and)
+    ts(c("PI", 4, 5), pi, 1, ALU.bitwise_and)
+    r8 = at(T.R8[0:8, :], 128, ("R8", 0, 128))
+    ts(r8, at(T.XG[0:8, :], 128, ("XG", 0, 128)), at(T.COL[0:8, 2:3], 1, ("COL", 2, 3)), ALU.is_equal)
+    ts(col(0), c("PI", 1, 2), 2.0, ALU.mult, -16.0, ALU.add)
+    cp(col(3), c("PI", 2, 3))
+    ts(col(4), c("PI", 2, 3), 16.0, ALU.mult, 15.0, ALU.add)
+    cp(col(5), c("PI", 3, 4))
+    ts(col(7), c("PI", 4, 5), -63.0, ALU.mult, 64.0, ALU.add)
+    ts(ID, c("XI", 0, 128), col(2), ALU.is_equal)
+    ts(BB, c("XG", 0, 128), col(3), ALU.is_equal)
+    ts(c("Z", 0, 144), c("XI", 0, 144), col(4), ALU.is_equal, HOLE, ALU.mult)
+    act(col(1), col(0), bias=-1.0)
+    act(col(6), col(5), scale=997.0)
+    act(col(8), col(7), bias=65.0, scale=-1.0)
+    act(NI, ID, scale=-1.0)
+    ts(c("COL", 12, 16), c("XT", 0, 4), col(5), ALU.is_equal, col(8), ALU.mult)
+    for t in range(RO):
+        act(sv(t), BB, scale=col(12 + t))
+
+    uf = at(T.UF[0:8, :], A, ("UF", 0, A))
+    cp(uf, at(T.UI[0:8, :], A, ("UI", 0, A)))
+    mm(c("V", 0, A), r8, uf)
+    idx1(0, A, c("SRI", 0, A))
+    cp(c("LIM0", 0, A), c("LMI", 0, A))
+    idx2(0, A)
+    spread("LIM0", H, 256, act)
+    spread("LIM0", 0, H)
+    ts(c("KA", 0, A), c("V", 0, A), col(6), ALU.add, col(7), ALU.mult)
+    ts(c("KB", 0, A), c("KA", 0, A), 6, ALU.arith_shift_right, 63, ALU.bitwise_and)
+    cp(c("KV0", 0, A), c("KB", 0, A))
+    by_vector(0, 64, 0, "PA")
+    by_scalar(256, 320, "LIM0", "PB")
+    by_vector(64, 128, 0, "PA")
+    drop(0, 128, c("SRI", 0, 128), "PA")
+    by_scalar(320, A, "LIM0", "PB")
+    by_vector(128, H, 0, "PC")
+    drop(128, H, c("SRI", 128, H), "PC")
+    tally(0, H)
+    drop(256, A, c("SRI", 256, A), "PB")
+    tally(256, A)
+    by_vector(H, 256, H, "PA")
+    drop(H, 256, c("SRI", H, 256), "PA")
+    tally(H, 256)
+
+    for t in range(RO - 1):
+        lo_, ln = "LIM%d" % (t % 2), "LIM%d" % ((t + 1) % 2)
+        ko, kn = "KV%d" % (t % 2), "KV%d" % ((t + 1) % 2)
+        order()
+        act(c(kn, 0, ST), pick(ko, 0, ST))
+        sort_s(H, A)
+        sort_s(0, H)
+        mm(c("V", 0, H), sv(t), c(kn, 0, H))
+        mm(c("V", H, ST), sv(t + 1), c(kn, H, ST))
+        act(c(ln, 0, H), pick(lo_, 0, H))
+        act(c(ln, H, ST), pick(lo_, H, ST))
+        idx1(0, H, rev("SS", H, A))
+        idx1(H, ST, c("SS", H, ST))
+        mm(c("V", 0, H), sv(t + 1), c(kn, 0, H))
+        idx2(0, ST)
+        for b in range(NB):
+            act(m1(t, b, 1), pick(lo_, ST + BK * b, ST + BK * (b + 1)))
+            act(m1(t, b, 2), pick(ko, ST + BK * b, ST + BK * (b + 1)))
+        act(at(T.M1[:, NB * t:NB * (t + 1), 0:BK], NB * BK, *[("M1", NB * t + b, NB * t + b + 0.25) for b in range(NB)]),
+            c("SS", ST, A))
+        send(1, t)
+        spread(ln, 0, 128)
+        spread4(ln, 128, H)
+        term_v(0, 128)
+        term_a(128, H)
+        by_vector(0, 96, 0, "PA", c("TM", 0, 96))
+        by_scalar(128, H, ln, "PB", c("TM", 128, H))
+        rob(0, 96, "PA", rev("M2", 96 * t, 96 * (t + 1)))
+        send(2, t)
+        by_vector(96, 128, 0, "PB", c("TM", 96, 128))
+        by_scalar(H, 256, ln, "PC")
+        rob(96, H, "PB", rev("SS", H, ST))
+        idx1(0, 96, c("SS", 0, 96))
+        idx2(0, 96)
+        idx1(96, H, c("SS", 96, H))
+        idx2(96, H)
+        act(c(kn, ST, A), landed(t, 2))
+        act(c(ln, ST, A), landed(t, 1))
+        mm(c("V", ST, A), sv(t + 1), c(kn, ST, A))
+        idx1(ST, A, landed(t, 0))
+        idx2(ST, A)
+        by_scalar(256, 320, ln, "PC")
+        by_vector(0, 64, 0, "PA")
+        by_vector(64, 128, 0, "PA")
+        drop(0, 128, c("SS", 0, 128), "PA")
+        drop(H, ST, c("SS", H, ST), "PC")
+        drop(ST, 320, c("L2", 96 * t, 96 * t + 32), "PC")
+        by_scalar(320, A, ln, "V")
+        by_vector(128, H, 128, "PB")
+        tally(0, 128)
+        drop(128, H, c("SS", 128, H), "PB")
+        tally(128, 320)
+        drop(320, A, c("L2", 96 * t + 32, 96 * (t + 1)), "V")
+        tally(320, A)
+
+    t = RO - 1
+    lo_, ln, ko, kn = "LIM1", "LIM0", "KV1", "KV0"
+    order()
+    act(c(kn, 0, 96), pick(ko, 0, 96))
+    sort_s(ST, A)
+    mm(c("V", 0, 96), sv(t), c(kn, 0, 96))
+    act(c(ln, 0, 96), pick(lo_, 0, 96))
+    sort_s(0, 96)
+    idx1(0, 96, rev("SS", ST, A))
+    idx2(0, 96)
+    act(c(kn, 96, ST), pick(ko, 96, ST))
+    mm(c("V", 96, H), sv(t), c(kn, 96, H))
+    spread4(ln, 0, 64)
+    term_v(0, 64)
+    term_a(64, 96)
+    for b in range(NB):
+        act(m1(t, b, 1), pick(lo_, ST + BK * b, ST + BK * (b + 1)))
+        act(m1(t, b, 2), pick(ko, ST + BK * b, ST + BK * (b + 1)))
+    send(1, t)
+    by_vector(0, 32, 0, "PA", c("TM", 0, 32))
+    by_scalar(64, 96, ln, "PC", c("TM", 64, 96))
+    by_vector(32, 64, 0, "PB", c("TM", 32, 64))
+    rob(0, 32, "PA", rev("M2", 96 * t + 64, 96 * t + 96))
+    rob(64, 96, "PC", rev("M2", 96 * t, 96 * t + 32))
+    rob(32, 64, "PB", rev("M2", 96 * t + 32, 96 * t + 64))
+    send(2, t)
+    sort_s(96, ST)
+    act(c(ln, 96, ST), pick(lo_, 96, ST))
+    idx1(96, H, rev("SS", H, ST))
+    idx2(96, H)
+    spread4(ln, 96, 160)
+    term_v(96, 160)
+    term_a(160, H)
+    by_scalar(160, H, ln, "PA", c("TM", 160, H), "D1")
+    by_vector(96, 160, 96, "PA", c("TM", 96, 160))
+    rob(96, H, "PA", rev("SS", H, ST))
+    act(c("OUTL", 0, ST), c(ln, 0, ST))
+    dma("s", hbm(T.ylim[:, 0:ST]), c("OUTL", 0, ST), 2400)
+    dma("s", hbm(T.ysr[:, 0:ST]), c("SS", 0, ST), 2400)
+    act(c(kn, ST, A), landed(t, 2))
+    v8 = at(T.V[0:8, 0:A], A, ("V", 0, A))
+    mm(v8, c("SV", 0, 128, 16), c(kn, 0, A))
+    k8 = at(T.OUTK[0:8, :], A, ("OUTK", 0, A))
+    act(k8, v8)
+    dma("s", hbm(T.ylim[:, ST:A]), landed(t, 1), 2000)
+    dma("a", hbm(T.yu[:]), k8, 1900)
+    dma("s", hbm(T.ysr[:, ST:A]), c("L2", 96 * t, 96 * (t + 1)), 2000)
+
+    ends = emit(g, T, arrange(nodes))
+    for name in ends:
+        g.wait_ge(T.sem[name], ends[name])
+    g.wait_ge(T.sem.sent, sent[0])

@@ -6,7 +6,10 @@ AF = ActivationFunctionType
 A, H, ST, BK, NB, RO, W = 384, 192, 288, 32, 3, 4, 4096
 HOLE = 4096.0
 BIG = 131072.0
-CFG = {"gam": 1.3, "sig": 3.2, "cyc": 0.83, "pe": 0.42, "hop": 80, "vfix": 20, "afix": 60, "riss": 800, "rlat": 2000}
+CFG = {"gam": 1.3, "sig": 3.2, "cyc": 0.83, "pe": 0.42, "hop": 160, "vfix": 20, "afix": 60, "riss": 800, "rlat": 2000,
+       "late": 1000, "tries": 8000, "moves": 2}
+CASES = [(1.0, 1.0, 0.0), (0.8, 1.0, 2000.0), (1.15, 1.3, 1000.0)]
+PLAN = {}
 
 
 def sb(n, dtype):
@@ -21,7 +24,7 @@ SCRATCH = {
     "CKD": sb(128, "bfloat16"), "CKA": sb(64, "bfloat16"), "SW": sb(A, "float32"), "SS": sb(A, "float32"),
     "LIM0": sb(A, "bfloat16"), "LIM1": sb(A, "bfloat16"), "KV0": sb(A, "bfloat16"), "KV1": sb(A, "bfloat16"),
     "PR": sb(A, "int32"), "CX": sb(A, "int32"), "CU": sb(A, "uint16"), "KA": sb(A, "int32"), "KB": sb(A, "int32"),
-    "LX": sb(16 * 256, "bfloat16"), "L4": sb(4 * 256, "bfloat16"),
+    "LX": sb(16 * A, "bfloat16"), "L4": sb(4 * A, "bfloat16"),
     "IND": sb(16 * A, "bfloat16"), "REC": sb(16 * A, "bfloat16"),
     "HS": sb(A, "bfloat16"), "JK": sb(A, "bfloat16"), "E": sb(A, "bfloat16"), "M": sb(A, "bfloat16"),
     "OW": sb(A, "bfloat16"), "BASE": sb(4, "float32"), "PL": sb(24, "uint16"), "OL": sb(24, "uint16"),
@@ -110,6 +113,8 @@ def clash(x, y, qx, qy):
 
 def arrange(nodes):
     n = len(nodes)
+    if n in PLAN:
+        return [o for k in PLAN[n] for o in nodes[k]["ops"]]
     pred = [dict() for _ in nodes]
     by_buf = {}
     for k, nd in enumerate(nodes):
@@ -131,23 +136,71 @@ def arrange(nodes):
     for k in range(n):
         for j in pred[k]:
             succ[j].append(k)
-    level = [0.0] * n
-    for k in range(n - 1, -1, -1):
-        level[k] = nodes[k]["busy"] + 0.001 + max([nodes[k]["lat"]] + [pred[s][k] + level[s] for s in succ[k]])
-    taken = {}
-    for k in sorted(range(n), key=lambda j: -level[j]):
-        nd = nodes[k]
-        start = max([0.0] + [nodes[j]["end"] + d for j, d in pred[k].items()])
-        if nd["q"]:
-            spans = taken.setdefault(nd["q"], [])
-            for lo, hi in spans:
-                if start + nd["busy"] <= lo:
-                    break
-                start = max(start, hi)
-            spans.append((start, start + nd["busy"]))
-            spans.sort()
-        nd["start"], nd["end"] = start, start + nd["busy"]
-    return [o for k in sorted(range(n), key=lambda j: (nodes[j]["start"], j)) for o in nodes[k]["ops"]]
+    pl = [list(p.items()) for p in pred]
+    busy = [nd["busy"] for nd in nodes]
+    qs = [nd["q"] for nd in nodes]
+    cases = []
+    for gather, other, late in CASES:
+        cases.append(([x * (gather if nd["ops"][0]["ind"] else other) for x, nd in zip(busy, nodes)],
+                      [late if q is None else 0.0 for q in qs]))
+
+    def place(extra):
+        level = [0.0] * n
+        for k in range(n - 1, -1, -1):
+            level[k] = busy[k] + extra[k] + 0.001 + max([nodes[k]["lat"]] + [pred[s][k] + level[s] for s in succ[k]])
+        taken = {}
+        start, end = [0.0] * n, [0.0] * n
+        for k in sorted(range(n), key=lambda j: -level[j]):
+            st = max([0.0] + [end[j] + d for j, d in pl[k]])
+            if qs[k]:
+                spans = taken.setdefault(qs[k], [])
+                i = len(spans)
+                while i and spans[i - 1][1] > st:
+                    i -= 1
+                while i < len(spans) and st + busy[k] > spans[i][0]:
+                    st = max(st, spans[i][1])
+                    i += 1
+                spans.insert(i, (st, st + busy[k]))
+            else:
+                st += CFG["late"]
+            start[k], end[k] = st, st + busy[k]
+        return sorted(range(n), key=lambda j: (start[j], j))
+
+    def length(seq):
+        total = 0.0
+        for bz, late in cases:
+            end = [0.0] * n
+            free = {}
+            top = 0.0
+            for k in seq:
+                st = free.get(qs[k], 0.0) if qs[k] else 0.0
+                for j, d in pl[k]:
+                    if end[j] + d > st:
+                        st = end[j] + d
+                end[k] = free[qs[k]] = st + bz[k] + late[k]
+                top = max(top, end[k] + nodes[k]["lat"])
+            total += top
+        return total
+
+    extra = [0.0] * n
+    seq = place(extra)
+    best = length(seq)
+    r = 1
+    for _ in range(CFG["tries"]):
+        other = list(extra)
+        r = (r * 1103515245 + 12345) % 2147483648
+        mid = (r >> 8) % n
+        for _ in range(CFG["moves"]):
+            r = (r * 1103515245 + 12345) % 2147483648
+            k = min(n - 1, mid + (r >> 8) % 40)
+            r = (r * 1103515245 + 12345) % 2147483648
+            other[k] = ((r >> 8) % 1000) * 1.5 if (r >> 20) % 3 else 0.0
+        s2 = place(other)
+        now = length(s2)
+        if now <= best:
+            best, extra, seq = now, other, s2
+    PLAN[n] = seq
+    return [o for k in seq for o in nodes[k]["ops"]]
 
 
 def emit(g, T, ops):
@@ -244,7 +297,8 @@ def rank_program(g, core, T, topo):
         for i in ins:
             if isinstance(i, tuple):
                 acc += [r + (False,) for r in i[3:]]
-        d = {"q": q, "fn": fn, "acc": acc}
+        d = {"q": q, "fn": fn, "acc": acc,
+             "ind": any(isinstance(x, tuple) and x[2] == "win" for x in list(outs) + list(ins))}
         d.update(kw)
         if join:
             nodes[-1]["ops"].append(d)
@@ -355,6 +409,10 @@ def rank_program(g, core, T, topo):
         k = NB * t + b
         return at(T.M1[:, k, part * BK:(part + 1) * BK], BK, ("M1", k + part / 4.0, k + (part + 1) / 4.0))
 
+    def m1all(t, part):
+        return at(T.M1[:, NB * t:NB * (t + 1), part * BK:(part + 1) * BK], NB * BK,
+                  *[("M1", NB * t + b + part / 4.0, NB * t + b + (part + 1) / 4.0) for b in range(NB)])
+
     ID, NI, BB = c("ID", 0, 128), c("NI", 0, 128), c("BB", 0, 128)
 
     def sel(r):
@@ -451,7 +509,7 @@ def rank_program(g, core, T, topo):
     dma("a", at(T.UI[0:8, :], A, ("UI", 0, A)), hbm(T.u[:]), 1900)
     k = dma("s", c("SRI", 0, A), hbm(T.sr[:]), 2600)
     k = dma("s", c("LMI", 0, A), hbm(T.lim[:]), 3300, [(k, 0)])
-    dma("s", c("FIT", 0, W), hbm(T.fit[:]), 7400, [(k, 0)])
+    dma("s", c("FIT", 0, W), hbm(T.fit[:]), 6000, [(k, 0)])
     iota(c("PI", 0, 1), [[0, 1]], 0, 1, False)
     iota(col(2), [[0, 1]], 0, 1, True)
     iota(c("XG", 0, 128), [[1, 8], [0, 16]], 0, 0, True)
@@ -511,26 +569,27 @@ def rank_program(g, core, T, topo):
     for t in range(RO - 1):
         lo_, ln = "LIM%d" % (t % 2), "LIM%d" % ((t + 1) % 2)
         ko, kn = "KV%d" % (t % 2), "KV%d" % ((t + 1) % 2)
+        mm(c("PA", 0, A), sv(t + 1), c(ko, 0, A))
+        tt(c("KA", 0, A), c("SW", 0, A), c("PA", 0, A), ALU.mult)
+        ts(c("KB", 0, A), c("KA", 0, A), 5, ALU.arith_shift_right, W - 1, ALU.bitwise_and)
         order()
-        act(c(kn, 0, ST), pick(ko, 0, ST))
+        act(c(kn, 0, H), pick(ko, 0, H))
+        cp(c("CU", H, A), pick("KB", H, A))
         sort_s(H, A)
         sort_s(0, H)
         mm(c("V", 0, H), sv(t), c(kn, 0, H))
-        mm(c("V", H, ST), sv(t + 1), c(kn, H, ST))
         act(c(ln, 0, H), pick(lo_, 0, H))
         act(c(ln, H, ST), pick(lo_, H, ST))
+        act(c(kn, H, ST), pick(ko, H, ST))
         idx1(0, H, rev("SS", H, A))
-        idx1(H, ST, c("SS", H, ST))
         mm(c("V", 0, H), sv(t + 1), c(kn, 0, H))
-        idx2(0, ST)
+        idx2(0, H)
+        cp(m1all(t, 0), c("CU", ST, A))
         for b in range(NB):
             act(m1(t, b, 1), pick(lo_, ST + BK * b, ST + BK * (b + 1)))
             act(m1(t, b, 2), pick(ko, ST + BK * b, ST + BK * (b + 1)))
-        act(at(T.M1[:, NB * t:NB * (t + 1), 0:BK], NB * BK, *[("M1", NB * t + b, NB * t + b + 0.25) for b in range(NB)]),
-            c("SS", ST, A))
         send(1, t)
         spread(ln, 0, 128)
-        spread4(ln, 128, H)
         term_v(0, 128)
         term_a(128, H)
         by_vector(0, 96, 0, "PA", c("TM", 0, 96))
@@ -540,27 +599,28 @@ def rank_program(g, core, T, topo):
         by_vector(96, 128, 0, "PB", c("TM", 96, 128))
         by_scalar(H, 256, ln, "PC")
         rob(96, H, "PB", rev("SS", H, ST))
+        give = len(nodes) - 2
         idx1(0, 96, c("SS", 0, 96))
         idx2(0, 96)
         idx1(96, H, c("SS", 96, H))
+        nodes[-1]["after"].append((give, 0))
         idx2(96, H)
-        act(c(kn, ST, A), landed(t, 2))
-        act(c(ln, ST, A), landed(t, 1))
-        mm(c("V", ST, A), sv(t + 1), c(kn, ST, A))
-        idx1(ST, A, landed(t, 0))
-        idx2(ST, A)
-        by_scalar(256, 320, ln, "PC")
+        by_scalar(128, H, ln, "PC")
         by_vector(0, 64, 0, "PA")
         by_vector(64, 128, 0, "PA")
+        cp(c("CU", ST, A), landed(t, 0))
+        act(c(ln, ST, A), landed(t, 1))
+        act(c(kn, ST, A), landed(t, 2))
+        spread4(ln, 320, A)
+        drop(128, 256, c("SS", 128, 256), "PC")
         drop(0, 128, c("SS", 0, 128), "PA")
-        drop(H, ST, c("SS", H, ST), "PC")
-        drop(ST, 320, c("L2", 96 * t, 96 * t + 32), "PC")
-        by_scalar(320, A, ln, "V")
-        by_vector(128, H, 128, "PB")
-        tally(0, 128)
-        drop(128, H, c("SS", 128, H), "PB")
-        tally(128, 320)
-        drop(320, A, c("L2", 96 * t + 32, 96 * (t + 1)), "V")
+        tally(0, 256)
+        by_scalar(256, 320, ln, "V")
+        by_vector(320, A, 320, "PB")
+        drop(256, ST, c("SS", 256, ST), "V")
+        drop(ST, 320, c("L2", 96 * t, 96 * t + 32), "V")
+        drop(320, A, c("L2", 96 * t + 32, 96 * (t + 1)), "PB")
+        tally(256, 320)
         tally(320, A)
 
     t = RO - 1

@@ -6,9 +6,35 @@ AF = ActivationFunctionType
 A, H, ST, BK, NB, RO, W = 384, 192, 288, 32, 3, 4, 4096
 HOLE = 4096.0
 BIG = 131072.0
-CFG = {"gam": 1.3, "sig": 3.2, "cyc": 0.83, "pe": 0.42, "hop": 160, "vfix": 20, "afix": 60, "riss": 800, "rlat": 2000,
-       "late": 1000, "tries": 8000, "moves": 2}
-CASES = [(1.0, 1.0, 0.0), (0.8, 1.0, 2000.0), (1.15, 1.3, 1000.0)]
+CFG = {"gam": 1.3, "sig": 3.2, "cyc": 0.83, "pe": 0.42, "hop": 160, "vfix": 20, "afix": 60, "riss": 700, "rlat": 1100,
+       "late": 300, "tries": 16000, "moves": 2, "tied": 0.9, "seed": 3, "aim": 0, "heat": 300.0,
+       "polish": 2000, "far": 4, "warm": 50.0}
+CASES = [(1.0, 1.0, 0.0), (0.8, 1.0, 1500.0), (1.33, 1.5, 0.0)]
+FIRST = [("v", 0, 64), ("a", 192, 256), ("v", 64, 128), ("a", 256, 320), ("v", 128, 192), ("v", 320, 384)]
+FIRSTSUM = [(0, 128, "PA"), (192, 256, "PB"), (128, 192, "PC"), (256, 320, "V"), (320, 384, "PA")]
+FIRSTWIDE = [(0, 128, 16, "v"), (128, 192, 16, "a"), (320, 384, 4, "gg")]
+LASTW = [(0, 32, 4, "vv"), (64, 96, 4, "aa"), (96, 128, 4, "gg")]
+LAST = [("v", 0, 32), ("v", 64, 96), ("a", 32, 64), ("a", 128, 192), ("v", 96, 128)]
+LASTSUM = [(0, 32, "PA"), (64, 96, "PC"), (32, 64, "PB"), (96, 192, "V")]
+LSORT = [("a", "K", 0, 96), ("v", "S", 288, 384), ("a", "L", 0, 96), ("a", "K", 96, 192), ("v", "S", 192, 288),
+         ("v", "S", 0, 96), ("a", "L", 96, 192), ("a", "S", 96, 192), ("a", "K", 192, 384), ("a", "O", 288, 384),
+         ("a", "O", 0, 288)]
+LPACK = "g"
+PACK = "ggggg"
+SORT = [("a", "K", 0, 192), ("v", "S", 192, 384), ("a", "L", 0, 192), ("a", "S", 0, 192), ("a", "L", 192, 384),
+        ("a", "K", 192, 384)]
+WIDE = [(0, 128, 16, "v"), (320, 384, 4, "gv")]
+TESTS = [("a", 192, 256), ("v", 0, 96), ("a", 128, 192), ("v", 96, 128), ("v", 384, 448), ("a", 512, 576),
+         ("v", 448, 512), ("a", 256, 320), ("v", 320, 352), ("v", 352, 384)]
+RING = ["D0", "D1", "H1", "H2"]
+MOVES = [(0, 96, "PA"), (96, 192, "V")]
+SUMS = [(0, 64, "PB"), (128, 192, "PC"), (64, 128, "PB")]
+DROPS = [(192, 256, "PB"), (256, 320, "V"), (320, 384, "PA")]
+TALLY = [(0, 128), (128, 256)]
+STAGES = [(0, 256, "D0", "D1"), (256, 384, "PC", "PB")]
+FIRSTSTAGES = [(0, 256, "H1", "H2"), (256, 384, "PC", "PB")]
+SCAN, WRAP = "H1", "H2"
+PAD = 16
 PLAN = {}
 
 
@@ -17,27 +43,30 @@ def sb(n, dtype):
 
 
 SCRATCH = {
-    "FIT": sb(W, "bfloat16"), "SRI": sb(A, "int32"), "LMI": sb(A, "int32"), "UI": sb(A, "int32"), "UF": sb(A, "float32"),
+    "FIT": sb(PAD + 2 * W, "bfloat16"), "SRI": sb(A, "int32"), "LMI": sb(A, "int32"), "UI": sb(A, "int32"), "UF": sb(A, "float32"),
     "XI": sb(144, "float32"), "XG": sb(128, "float32"), "XT": sb(4, "float32"), "PI": sb(8, "int32"),
-    "COL": sb(16, "float32"), "NUM": sb(A, "bfloat16"), "ID": sb(128, "bfloat16"), "NI": sb(128, "bfloat16"),
+    "COL": sb(24, "float32"), "NUM": sb(A, "bfloat16"), "ID": sb(128, "bfloat16"), "NI": sb(128, "bfloat16"),
+    "HV": sb(128, "bfloat16"), "HA": sb(128, "bfloat16"), "IB": sb(128, "bfloat16"), "NH": sb(128, "bfloat16"), "NB": sb(128, "bfloat16"),
     "Z": sb(144, "bfloat16"), "BB": sb(128, "bfloat16"), "SV": sb(512, "bfloat16"), "R8": sb(128, "float32"),
-    "CKD": sb(128, "bfloat16"), "CKA": sb(64, "bfloat16"), "SW": sb(A, "float32"), "SS": sb(A, "float32"),
+    "CK": sb(7 * H, "bfloat16"), "SW": sb(A, "float32"), "SS": sb(A, "float32"),
     "LIM0": sb(A, "bfloat16"), "LIM1": sb(A, "bfloat16"), "KV0": sb(A, "bfloat16"), "KV1": sb(A, "bfloat16"),
-    "PR": sb(A, "int32"), "CX": sb(A, "int32"), "CU": sb(A, "uint16"), "KA": sb(A, "int32"), "KB": sb(A, "int32"),
-    "LX": sb(16 * A, "bfloat16"), "L4": sb(4 * A, "bfloat16"),
-    "IND": sb(16 * A, "bfloat16"), "REC": sb(16 * A, "bfloat16"),
-    "HS": sb(A, "bfloat16"), "JK": sb(A, "bfloat16"), "E": sb(A, "bfloat16"), "M": sb(A, "bfloat16"),
+    "PR": sb(A, "int32"), "CX": sb(A, "int32"), "CY": sb(H, "int32"), "CU": sb(A + H, "uint16"),
+    "KA": sb(A, "int32"), "KB": sb(A, "int32"), "KC": sb(A, "int32"),
+    "LX": sb(16 * A, "bfloat16"), "L4": sb(8 * A, "bfloat16"),
+    "IND": sb(16 * (A + ST), "bfloat16"), "REC": sb(16 * (A + H), "bfloat16"),
+    "HS": sb(A, "bfloat16"), "JK": sb(A, "bfloat16"), "E": sb(A + 2, "bfloat16"), "M": sb(A, "bfloat16"),
     "OW": sb(A, "bfloat16"), "BASE": sb(4, "float32"), "PL": sb(24, "uint16"), "OL": sb(24, "uint16"),
-    "TM": sb(H, "bfloat16"),
-    "M1": ("sbuf", [128, RO * NB, 3 * BK], "float32"), "L1": ("sbuf", [128, RO * NB, 3 * BK], "float32"),
-    "M2": sb(RO * NB * BK, "float32"), "L2": sb(RO * NB * BK, "float32"),
-    "OUTL": sb(ST, "float32"), "OUTK": sb(A, "float32"),
+    "TM": sb(H, "bfloat16"), "MV": sb(RO * H, "bfloat16"),
+    "M1": ("sbuf", [128, RO * NB, 4 * BK], "float32"), "L1": ("sbuf", [128, RO * NB, 4 * BK], "float32"),
+    "L2": sb(RO * NB * BK, "bfloat16"), "L3": sb(NB * BK, "float32"),
+    "OUTL": sb(A, "float32"), "OUTK": sb(A, "float32"),
 }
 for bank_ in ("D0", "D1", "PA", "PB", "PC", "V", "H1", "H2"):
     SCRATCH[bank_] = ("psum", [128, 512], "float32")
 NDMA = 12
 SEMAPHORES = (["q_v", "q_a", "q_p", "q_g", "sent"] + ["dm%d" % k for k in range(NDMA)]
-              + ["a1_%d" % t for t in range(RO)] + ["a2_%d" % t for t in range(RO)])
+              + ["a%d_%d" % (kd, t) for kd in (1, 2) for t in range(RO)])
+BARS = [-11, -7, -41, -35, 5, 9, 1]
 
 
 def routes(T, topo):
@@ -76,18 +105,25 @@ def relay_masks(T, topo, rt, r):
     return out
 
 
-def piece(T, kind, land, t, b):
+def place_of(kind, land, t, b):
+    k = NB * t + b
     if kind == 1:
-        lo = BK if t == RO - 1 else 0
-        return T["L1" if land else "M1"][:, NB * t + b, lo:3 * BK]
-    c = (NB * t + b) * BK
-    return T["L2" if land else "M2"][:, c:c + BK]
+        return ("L1" if land else "M1", k, k + 1)
+    if t < RO - 1:
+        return ("L2", BK * k, BK * (k + 1)) if land else ("MV", H * t + ST - H + BK * b, H * t + ST - H + BK * (b + 1))
+    return ("L3", BK * b, BK * (b + 1)) if land else ("SW", ST + BK * b, ST + BK * (b + 1))
+
+
+def piece(T, kind, land, t, b):
+    name, lo, hi = place_of(kind, land, t, b)
+    if kind == 1:
+        return T[name][:, lo, (2 * BK if t == RO - 1 else 0):4 * BK]
+    return T[name][:, lo:hi]
 
 
 def relay_program(g, core, T, topo, rt):
-    mine = [k for k in rt if rt[k][1] == core]
     total = 0
-    for (r, b) in mine:
+    for (r, b) in [k for k in rt if rt[k][1] == core]:
         dst = rt[(r, b)][0]
         n_in = len(relay_masks(T, topo, rt, r)[b])
         rid, pid = topo.addr(dst, core)
@@ -111,10 +147,7 @@ def clash(x, y, qx, qy):
     return (x[3] or y[3]) and x[1] < y[2] and y[1] < x[2]
 
 
-def arrange(nodes):
-    n = len(nodes)
-    if n in PLAN:
-        return [o for k in PLAN[n] for o in nodes[k]["ops"]]
+def depends(nodes):
     pred = [dict() for _ in nodes]
     by_buf = {}
     for k, nd in enumerate(nodes):
@@ -132,26 +165,50 @@ def arrange(nodes):
             pred[k][j] = max(pred[k].get(j, 0), d)
         for x in acc:
             by_buf.setdefault(x[0], []).append((k, x))
-    succ = [[] for _ in nodes]
-    for k in range(n):
-        for j in pred[k]:
-            succ[j].append(k)
+    far = [set() for _ in nodes]
+    for k in range(len(nodes)):
+        for j in sorted(pred[k], reverse=True):
+            if j in far[k] and nodes[j]["lat"] == 0 and pred[k][j] <= CFG["hop"] and nodes[j]["q"] is not None:
+                del pred[k][j]
+            else:
+                far[k] |= far[j]
+                far[k].add(j)
+    return pred
+
+
+def arrange(nodes):
+    n = len(nodes)
+    if n in PLAN:
+        return [o for k in PLAN[n] for o in nodes[k]["ops"]]
+    pred = depends(nodes)
     pl = [list(p.items()) for p in pred]
+    sl = [[] for _ in nodes]
+    for k in range(n):
+        for j, d in pl[k]:
+            sl[j].append((k, d))
     busy = [nd["busy"] for nd in nodes]
     qs = [nd["q"] for nd in nodes]
+    tail = [nd["lat"] for nd in nodes]
     cases = []
     for gather, other, late in CASES:
-        cases.append(([x * (gather if nd["ops"][0]["ind"] else other) for x, nd in zip(busy, nodes)],
-                      [late if q is None else 0.0 for q in qs]))
+        cases.append([x * (gather if nd["ops"][0]["ind"] else other) + (late if nd["q"] is None else 0.0)
+                      for x, nd in zip(busy, nodes)])
 
     def place(extra):
         level = [0.0] * n
         for k in range(n - 1, -1, -1):
-            level[k] = busy[k] + extra[k] + 0.001 + max([nodes[k]["lat"]] + [pred[s][k] + level[s] for s in succ[k]])
+            top = tail[k]
+            for s, d in sl[k]:
+                if d + level[s] > top:
+                    top = d + level[s]
+            level[k] = busy[k] + extra[k] + 0.001 + top
         taken = {}
         start, end = [0.0] * n, [0.0] * n
         for k in sorted(range(n), key=lambda j: -level[j]):
-            st = max([0.0] + [end[j] + d for j, d in pl[k]])
+            st = 0.0
+            for j, d in pl[k]:
+                if end[j] + d > st:
+                    st = end[j] + d
             if qs[k]:
                 spans = taken.setdefault(qs[k], [])
                 i = len(spans)
@@ -168,7 +225,7 @@ def arrange(nodes):
 
     def length(seq):
         total = 0.0
-        for bz, late in cases:
+        for bz in cases:
             end = [0.0] * n
             free = {}
             top = 0.0
@@ -177,28 +234,105 @@ def arrange(nodes):
                 for j, d in pl[k]:
                     if end[j] + d > st:
                         st = end[j] + d
-                end[k] = free[qs[k]] = st + bz[k] + late[k]
-                top = max(top, end[k] + nodes[k]["lat"])
+                end[k] = free[qs[k]] = st + bz[k]
+                if end[k] + tail[k] > top:
+                    top = end[k] + tail[k]
             total += top
         return total
 
+    def held(seq, bz):
+        end, why = [0.0] * n, [None] * n
+        last = {}
+        for k in seq:
+            j0 = last.get(qs[k]) if qs[k] else None
+            st = 0.0
+            for j, d in pl[k]:
+                if end[j] + d > st:
+                    st, why[k] = end[j] + d, (j, False)
+            if j0 is not None and end[j0] > st:
+                st, why[k] = end[j0], (j0, True)
+            end[k] = st + bz[k]
+            last[qs[k]] = k
+        k = max(range(n), key=lambda j: end[j] + tail[j])
+        out = []
+        while why[k]:
+            if why[k][1]:
+                out.append((why[k][0], k))
+            k = why[k][0]
+        return out
+
+    twins = {}
+    for k, nd in enumerate(nodes):
+        twins.setdefault(nd["twin"], []).append(k)
     extra = [0.0] * n
     seq = place(extra)
     best = length(seq)
-    r = 1
-    for _ in range(CFG["tries"]):
+    pairs = [p for bz in cases for p in held(seq, bz)]
+    seed = [CFG["seed"]]
+
+    def draw(m):
+        seed[0] = (seed[0] * 1103515245 + 12345) % 2147483648
+        return (seed[0] >> 8) % m
+
+    for step in range(CFG["tries"]):
         other = list(extra)
-        r = (r * 1103515245 + 12345) % 2147483648
-        mid = (r >> 8) % n
-        for _ in range(CFG["moves"]):
-            r = (r * 1103515245 + 12345) % 2147483648
-            k = min(n - 1, mid + (r >> 8) % 40)
-            r = (r * 1103515245 + 12345) % 2147483648
-            other[k] = ((r >> 8) % 1000) * 1.5 if (r >> 20) % 3 else 0.0
+        aim = draw(100) < CFG["aim"]
+        mid = pairs[draw(len(pairs))] if aim else [draw(n)] * 2
+        for move in range(CFG["moves"]):
+            if aim and move == 0:
+                up = draw(2)
+                k = mid[up]
+                to = extra[k] + draw(800) if up else max(-busy[k], extra[k] - draw(800))
+            else:
+                k = min(n - 1, max(0, mid[0] + draw(40) - 20))
+                to = draw(1000) * 1.5 if draw(3) else 0.0
+            for j in (twins[nodes[k]["twin"]] if step < CFG["tied"] * CFG["tries"] else [k]):
+                other[j] = to
+            if aim and draw(2):
+                break
         s2 = place(other)
         now = length(s2)
-        if now <= best:
+        if now <= best + CFG["heat"] * (1.0 - step / CFG["tries"]) * draw(100) / 100.0:
             best, extra, seq = now, other, s2
+            pairs = [p for bz in cases for p in held(seq, bz)]
+
+    up, down = [0] * n, [0] * n
+    for k in range(n):
+        for j, d in pl[k]:
+            up[k] |= up[j] | 1 << j
+    for k in range(n - 1, -1, -1):
+        for j, d in sl[k]:
+            down[k] |= down[j] | 1 << j
+
+    def shift(seq, j, k, early):
+        a, b = seq.index(j), seq.index(k)
+        if a > b or up[k] >> j & 1:
+            return seq
+        span = seq[a:b + 1]
+        mask = up[k] | 1 << k if early else ~(down[j] | 1 << j)
+        return seq[:a] + [x for x in span if mask >> x & 1] + [x for x in span if not mask >> x & 1] + seq[b + 1:]
+
+    keep = (best, seq)
+    for step in range(CFG["polish"]):
+        j, k = pairs[draw(len(pairs))]
+        back, early = draw(CFG["far"]), draw(2)
+        if early:
+            ahead = [x for x in seq[:seq.index(j) + 1] if qs[x] == qs[k]]
+            j = ahead[max(0, len(ahead) - 1 - back)]
+        else:
+            behind = [x for x in seq[seq.index(k):] if qs[x] == qs[k]]
+            k = behind[min(len(behind) - 1, back)]
+        s2 = seq
+        tj, tk = twins[nodes[j]["twin"]], twins[nodes[k]["twin"]]
+        for x, y in (zip(tj, tk) if len(tj) == len(tk) and tj.index(j) == tk.index(k) else [(j, k)]):
+            s2 = shift(s2, x, y, early)
+        now = length(s2)
+        if now <= best + CFG["warm"] * (1.0 - step / CFG["polish"]) * draw(100) / 100.0:
+            best, seq = now, s2
+            pairs = [p for bz in cases for p in held(seq, bz)]
+            if best < keep[0]:
+                keep = (best, seq)
+    seq = keep[1]
     PLAN[n] = seq
     return [o for k in seq for o in nodes[k]["ops"]]
 
@@ -241,10 +375,12 @@ def emit(g, T, ops):
             by_buf.setdefault(x[0], []).append((k, x))
     count = {q: 0 for q in eng}
     ends = {}
+    waited = {}
     for op in ops:
         q = op["q"]
         for j in op["waits"]:
             eng[q].wait_ge(T.sem[ops[j]["sem"]], ops[j]["val"])
+            waited[ops[j]["sem"]] = max(waited.get(ops[j]["sem"], 0), ops[j]["val"])
         if q is None:
             ends[op["sem"]] = op["val"]
             continue
@@ -252,25 +388,35 @@ def emit(g, T, ops):
         if op.get("remote"):
             continue
         if op.get("sem") is not None:
-            ins.then_inc(T.sem[op["sem"]], 16)
+            for i in ins:
+                i.then_inc(T.sem[op["sem"]], 16)
             ends[op["sem"]] = op["val"]
         elif op["marked"]:
             count[q] += 1
             op["sem"], op["val"] = "q_" + q, count[q]
             ins.then_inc(T.sem[op["sem"]], 1)
             ends[op["sem"]] = count[q]
-    return ends
+    return {name: ends[name] for name in ends if waited.get(name, 0) < ends[name]}
 
 
 def rank_program(g, core, T, topo):
     rt = routes(T, topo)
-    rank = T.rank_of(core)
-    if rank is None:
+    if T.rank_of(core) is None:
         relay_program(g, core, T, topo, rt)
         return
+    nodes, sent = calls(g, core, T, topo, rt)
+    ends = emit(g, T, arrange(nodes))
+    for name in ends:
+        g.wait_ge(T.sem[name], ends[name])
+    g.wait_ge(T.sem.sent, sent)
+
+
+def calls(g, core, T, topo, rt):
+    rank = T.rank_of(core)
     nodes = []
     ndma = [0]
     sent = [0]
+    back = [0]
     V, S, P = g.vector, g.scalar, g.tensor
     cyc = CFG["cyc"]
 
@@ -281,11 +427,15 @@ def rank_program(g, core, T, topo):
         ap = T[name][:, lo:hi:step] if step != 1 else T[name][:, lo:hi]
         return at(ap, len(range(lo, hi, step)), (name, lo, hi))
 
+    def rows(name, p0, p1, lo, hi):
+        return at(T[name][p0:p1, lo:hi], hi - lo, (name, lo, hi))
+
     def rev(name, lo, hi):
         return at(T[name][:, hi - 1:lo - 1:-1] if lo > 0 else T[name][:, hi - 1::-1], hi - lo, (name, lo, hi))
 
     def win(name, n, off, lo, hi):
-        return (T[name][:, 0:n].indirect(T[off][:, lo:hi]), 16 * (hi - lo), "win", (name, 0, n), (off, lo, hi))
+        a, b = n if isinstance(n, tuple) else (0, n)
+        return (T[name][:, a:b].indirect(T[off][:, lo:hi]), 16 * (hi - lo), "win", (name, a, b), (off, lo, hi))
 
     def op(q, fn, outs, ins, busy, lat=0.0, join=False, after=(), **kw):
         acc = []
@@ -304,7 +454,8 @@ def rank_program(g, core, T, topo):
             nodes[-1]["ops"].append(d)
             nodes[-1]["busy"] += busy
         else:
-            nodes.append({"q": q, "ops": [d], "busy": busy, "lat": lat, "after": list(after)})
+            nodes.append({"q": q, "ops": [d], "busy": busy, "lat": lat, "after": list(after),
+                          "twin": len(nodes) - back[0]})
         return len(nodes) - 1
 
     def val(x):
@@ -326,7 +477,8 @@ def rank_program(g, core, T, topo):
             op("v", lambda: V.tensor_scalar(out[0], in0[0], val(s1), val(s2), op0, op1), [out], [in0, s1, s2], vcost(out, in0))
 
     def tt(out, in0, in1, o):
-        op("v", lambda: V.tensor_tensor(out[0], in0[0], in1[0], o), [out], [in0, in1], vcost(out, in0, 1.0))
+        per = 2.0 if in0[2][0] == "sbuf" and in1[2][0] == "sbuf" else 1.0
+        op("v", lambda: V.tensor_tensor(out[0], in0[0], in1[0], o), [out], [in0, in1], vcost(out, in0, per))
 
     def cp(out, in_):
         op("v", lambda: V.tensor_copy(out[0], in_[0]), [out], [in_], vcost(out, in_))
@@ -344,18 +496,19 @@ def rank_program(g, core, T, topo):
         op("p", lambda: P.matmul(out[0], lhsT[0], rhs[0], start, stop), [out], [lhsT, rhs],
            max(64, rhs[1]) * CFG["pe"] * (1 if rhs[2][1] else 4), join=join)
 
-    def dma(q, out, in_, lat, after=()):
+    def dma(q, pairs, lat, after=()):
         e = g.sync if q == "s" else g.scalar
         name = "dm%d" % ndma[0]
         ndma[0] += 1
-        return op(q, lambda: e.dma_start(out[0], in_[0]), [out], [in_], 60, lat, after=after, sem=name, val=16)
+        return op(q, lambda: [e.dma_start(o[0], i[0]) for o, i in pairs], [o for o, i in pairs], [i for o, i in pairs],
+                  60 * len(pairs), lat, after=after, sem=name, val=16 * len(pairs))
 
     def hbm(ap):
         return (ap, 0, "hbm")
 
-    def iota(out, pattern, base, cm, small):
+    def iota(out, pattern, base, cm=0):
         busy = 130 + 2 * out[1] * cyc
-        if small:
+        if SCRATCH[out[3][0]][2] != "int32":
             op("g", lambda: g.iota(out[0], pattern, base, cm, allow_small_or_imprecise_dtypes=True), [out], [], busy)
         else:
             op("g", lambda: g.iota(out[0], pattern, base, cm), [out], [], busy)
@@ -363,26 +516,23 @@ def rank_program(g, core, T, topo):
     def col(k):
         return c("COL", k, k + 1)
 
-    def region(kd, land, t, b):
-        if kd == 1:
-            return at(None, 0, ("L1" if land else "M1", NB * t + b, NB * t + b + 1))
-        return at(None, 0, ("L2" if land else "M2", (NB * t + b) * BK, (NB * t + b + 1) * BK))
-
     rm = relay_masks(T, topo, rt, rank)
     chain = []
 
     def send(kd, t):
-        sem = T.sem["a%d_%d" % (kd, t)]
+        name = "a%d_%d" % (kd, t)
+        sem = T.sem[name]
         trs = []
         edges = []
         for b in rm:
             rid, pid = topo.addr(rt[(rank, b)][1], core)
-            trs.append(RemoteDMATransfer(dst_ids=[DstId(rid=rid, pnc=pid)], dma_engine_mask=bits(rm[b]),
-                                         remote_sem=sem, src=piece(T, kd, False, t, b), dst=piece(T, kd, True, t, b)))
+            trs.append(RemoteDMATransfer(dst_ids=[DstId(rid=rid, pnc=pid)], dma_engine_mask=bits(rm[b]), remote_sem=sem,
+                                         src=piece(T, kd, False, t, b), dst=piece(T, kd, True, t, b)))
             sent[0] += len(rm[b])
         if trs:
             k = op("g", lambda: g.remote_dma_fused(trs, local_sem=T.sem.sent), [],
-                   [region(kd, False, t, b) for b in rm], CFG["riss"], after=chain[-1:], remote=True)
+                   [at(None, 0, place_of(kd, False, t, b)) for b in rm], CFG["riss"], after=chain[-1:], remote=True,
+                   relayed=(kd, t))
             chain.append((k, 0))
             edges.append((k, 2 * CFG["rlat"] + CFG["riss"] + 2 * CFG["hop"]))
         for b in range(NB):
@@ -393,27 +543,20 @@ def rank_program(g, core, T, topo):
             sent[0] += len(topo.engines(core, dst))
             k = op("g", lambda b=b, dst=dst, rid=rid, pid=pid: g.remote_dma(
                 piece(T, kd, True, t, b), piece(T, kd, False, t, b), sem, T.sem.sent, pid, rid,
-                topo.mask(core, dst)), [], [region(kd, False, t, b)], CFG["riss"], remote=True)
+                topo.mask(core, dst)), [], [at(None, 0, place_of(kd, False, t, b))], CFG["riss"], remote=True)
             edges.append((k, CFG["rlat"]))
         n = 0
         for (r, b), (dst, via) in rt.items():
             if dst == core:
                 n += len(topo.engines(via if via is not None else T.cores[r], core))
-        op(None, None, [region(kd, True, t, b) for b in range(NB)], [], 0, after=edges,
-           sem="a%d_%d" % (kd, t), val=n)
+        op(None, None, [at(None, 0, place_of(kd, True, t, b)) for b in range(NB)], [], 0, after=edges, sem=name, val=n)
 
-    def landed(t, part):
-        return at(T.L1[:, NB * t:NB * (t + 1), part * BK:(part + 1) * BK], NB * BK, ("L1", NB * t, NB * (t + 1)))
+    def msg(name, t, part, b0=0, b1=NB):
+        k = NB * t
+        return at(T[name][:, k + b0:k + b1, part * BK:(part + 1) * BK], (b1 - b0) * BK,
+                  *[(name, k + b + part / 4.0, k + b + (part + 1) / 4.0) for b in range(b0, b1)])
 
-    def m1(t, b, part):
-        k = NB * t + b
-        return at(T.M1[:, k, part * BK:(part + 1) * BK], BK, ("M1", k + part / 4.0, k + (part + 1) / 4.0))
-
-    def m1all(t, part):
-        return at(T.M1[:, NB * t:NB * (t + 1), part * BK:(part + 1) * BK], NB * BK,
-                  *[("M1", NB * t + b + part / 4.0, NB * t + b + (part + 1) / 4.0) for b in range(NB)])
-
-    ID, NI, BB = c("ID", 0, 128), c("NI", 0, 128), c("BB", 0, 128)
+    ID, NI, IB, NB_, NH, BB = [c(n, 0, 128) for n in ("ID", "NI", "IB", "NB", "NH", "BB")]
 
     def sel(r):
         return c("Z", 15 - r, 143 - r)
@@ -421,257 +564,322 @@ def rank_program(g, core, T, topo):
     def sv(t):
         return c("SV", 128 * t, 128 * (t + 1))
 
-    def spread(lim, lo, hi, on=None):
-        for i in range(16):
-            (on or cp)(at(T.LX[:, 16 * lo + i:16 * hi:16], hi - lo, ("LX", 16 * lo + i / 32.0, 16 * lo + (i + 1) / 32.0)),
-                       c(lim, lo, hi))
+    def copy(on, out, in_):
+        if on == "g":
+            op("g", lambda: g.affine_select(out[0], in_[0], [[0, out[1]]], ALU.is_ge, 0.0, 0, 0), [out], [in_],
+               170 + 2 * out[1] * cyc)
+        else:
+            (cp if on == "v" else act)(out, in_)
 
-    def spread4(lim, lo, hi):
-        for j in range(4):
-            cp(at(T.L4[:, 4 * lo + j:4 * hi:4], hi - lo, ("L4", 4 * lo + j / 8.0, 4 * lo + (j + 1) / 8.0)), c(lim, lo, hi))
-        for j in range(4):
-            cp(at(T.LX[:, 16 * lo + j:16 * hi:4], 4 * (hi - lo), ("LX", 16 * lo + j / 32.0, 16 * lo + (j + 1) / 32.0)),
-               at(T.L4[:, 4 * lo:4 * hi], 4 * (hi - lo), ("L4", 4 * lo, 4 * lo + 1)))
+    def spread(src, lo, hi, k, on):
+        mid, m = ("LX" if k == 16 else "L4"), 16 // k
+        for j in range(k):
+            copy(on[0], at(T[mid][:, k * lo + j:k * hi:k], hi - lo, (mid, k * lo + j / 32.0, k * lo + (j + 1) / 32.0)),
+                 c(src, lo, hi) if isinstance(src, str) else src)
+        for j in range(m if m > 1 else 0):
+            copy(on[1 + j % (len(on) - 1)],
+                 at(T.LX[:, 16 * lo + j:16 * hi:m], k * (hi - lo), ("LX", 16 * lo + j / 32.0, 16 * lo + (j + 1) / 32.0)),
+                 at(T.L4[:, k * lo:k * hi], k * (hi - lo), ("L4", k * lo, k * lo + 1)))
 
-    def idx1(lo, hi, s):
-        tt(c("PR", lo, hi), s, c("V", lo, hi), ALU.mult)
-
-    def idx2(lo, hi):
+    def numbers(lo, hi):
         ts(c("CX", lo, hi), c("PR", lo, hi), 5, ALU.arith_shift_right, W - 1, ALU.bitwise_and)
-        cp(c("CU", lo, hi), c("CX", lo, hi))
 
-    def by_vector(lo, hi, part, bank, term=None):
-        lx = at(T.LX[:, 16 * lo:16 * hi], 16 * (hi - lo), ("LX", 16 * part, 16 * part + 1))
-        tt(c("IND", 16 * lo, 16 * hi), win("FIT", W, "CU", lo, hi), lx, ALU.is_gt)
-        mm(c(bank, lo, hi), ID, term or c("CKD", 0, hi - lo), True, False)
-        for i in range(16):
-            mm(c(bank, lo, hi), sel(i), c("IND", 16 * lo + i, 16 * hi, 16), False, i == 15, join=i != 0)
+    shape = {}
 
-    def by_scalar(lo, hi, lim, bank, term=None, one="D0"):
-        n = hi - lo
-        parts = [("D0", 0, 8), ("D1", 8, 16)] if n > 32 else [(one, 0, 16)]
-        act(c("REC", 16 * lo, 16 * hi), win("FIT", W, "CU", lo, hi))
-        for d, i0, i1 in parts:
-            for i in range(i0, i1):
-                mm(c(d, (i - i0) * n, (i - i0 + 1) * n), NI, c(lim, lo, hi), i == i0, False, join=i != i0)
-            for i in range(i0, i1):
-                mm(c(d, (i - i0) * n, (i - i0 + 1) * n), ID, c("REC", 16 * lo + i, 16 * hi, 16), False, i == i1 - 1,
-                   join=i != i0)
-            act(c("IND", 16 * lo + i0 * n, 16 * lo + i1 * n), c(d, 0, (i1 - i0) * n), AF.Sign, bias=-0.5)
-        mm(c(bank, lo, hi), ID, term or c("CKA", 0, n), True, False)
-        for d, i0, i1 in parts:
-            for i in range(i0, i1):
-                mm(c(bank, lo, hi), sel(i), c("IND", 16 * lo + i * n, 16 * lo + (i + 1) * n), False, i == 15, join=i != i0)
+    ring = ["D0", "D1"]
 
-    def drop(lo, hi, s, bank):
-        tt(c("SW", lo, hi), s, c(bank, lo, hi), ALU.max)
+    def test(on, lo, hi, lim, wides, span=(PAD, PAD + W)):
+        n, a = hi - lo, lo % A
+        for j in range(lo, hi):
+            shape[j] = (on, lo, hi)
+        if on == "v":
+            part = max(p for p, q in wides if p <= a)
+            tt(c("IND", 16 * lo, 16 * hi), win("FIT", span, "CU", lo, hi),
+               at(T.LX[:, 16 * a:16 * (a + n)], 16 * n, ("LX", 16 * part, 16 * part + 1)), ALU.is_gt)
+            return
+        act(c("REC", 16 * lo, 16 * hi), win("FIT", span, "CU", lo, hi))
+        sides = [(lo, c(lim, a, a + n))]
+        if on == "m":
+            sides.insert(0, (A + lo, rev(lim, A - hi, A - lo)))
+        for to, limits in sides:
+            banks = [ring.pop(0) for _ in range(2 if n > 32 else 1)]
+            ring.extend(banks)
+            for j in range(to, to + n):
+                shape[j] = ("a", to, to + n)
+            k = 16 // len(banks)
+            for h, d in enumerate(banks):
+                for i in range(k):
+                    mm(c(d, i * n, (i + 1) * n), NI, limits, i == 0, False, join=i > 0)
+                for i in range(k):
+                    mm(c(d, i * n, (i + 1) * n), ID, c("REC", 16 * lo + h * k + i, 16 * hi, 16), False, i == k - 1,
+                       join=i > 0)
+                act(c("IND", 16 * to + h * k * n, 16 * to + (h + 1) * k * n), c(d, 0, k * n), AF.Sign, bias=-0.5)
 
-    def tally(lo, hi):
-        act(c("HS", lo, hi), c("SW", lo, hi), AF.Sign, bias=-(HOLE - 0.5))
-        mm(c("H2", lo, hi), BB, c("HS", lo, hi))
-        mm(c("H1", lo, hi), BB, c("HS", lo, hi))
+    def alike(lo, hi):
+        cuts = [lo] + [j for j in range(lo + 1, hi) if shape[j] != shape[j - 1] and "a" in (shape[j][0], shape[j - 1][0])] + [hi]
+        return list(zip(cuts, cuts[1:]))
+
+    def total(lo, hi, bank, bar, first=(), last=()):
+        cuts = alike(lo, hi)
+        for j, (p, q) in enumerate(cuts):
+            k = H * BARS.index(bar[shape[p][0] == "a"])
+            mm(c(bank, p % A, p % A + q - p), ID, c("CK", k, k + q - p), j == 0, False, join=j > 0)
+        for a, b, st, mv in first:
+            mm(c(bank, a, b), st, mv, False, False)
+        for j, (p, q) in enumerate(cuts):
+            on, l0, h0 = shape[p]
+            for i in range(16):
+                src = c("IND", 16 * p + i, 16 * q, 16) if on == "v" else \
+                    c("IND", 16 * l0 + i * (h0 - l0) + p - l0, 16 * l0 + i * (h0 - l0) + q - l0)
+                mm(c(bank, p % A, p % A + q - p), sel(i), src, False,
+                   i == 15 and j == len(cuts) - 1 and not last,
+                   join=i % (16 if on == "v" else 8) > 0)
+        for j, (a, b, st, mv) in enumerate(last):
+            mm(c(bank, a, b), st, mv, False, j == len(last) - 1)
+
+    def tally(lo, hi, src="SW"):
+        act(c("HS", lo, hi), c(src, lo, hi), AF.Sign, bias=-(HOLE - 0.5))
+
+    def classes(stages):
+        for j, (lo, hi, b1, b2) in enumerate(stages):
+            mm(c(b2, lo, hi), BB, c("HS", lo, hi))
+            mm(c(b1, lo, hi), BB, c("HS", lo, hi))
+            ts(c("E", 2 + lo, 2 + hi), c(b1, lo, hi), 14.0, ALU.min, col(0), ALU.is_equal)
+            act(c("JK", lo, hi), c(b2, lo, hi), AF.Sign, bias=col(1), scale=-1.0, accum=c("BASE", 1 - j, 2 - j))
+            if j == 0:
+                act(c("E", 1, 2), c("BASE", 1, 2), scale=0.5)
 
     def wrap(src, bank):
         for r in range(16):
             mm(c(bank, 0, 24), sel(r), c(src, r, A, 16), r == 0, r == 15, join=r != 0)
 
     def order():
-        ts(c("E", 0, A), c("H1", 0, A), 14.0, ALU.min, col(0), ALU.is_equal)
-        act(c("JK", 0, A), c("H2", 0, A), AF.Sign, bias=col(1), scale=-1.0, accum=c("BASE", 0, 1))
-        e, st = c("E", 0, A), c("D0", 0, A)
+        e, st = c("E", 1, A + 2), c(SCAN, 1, A + 2)
         op("v", lambda: V.tensor_tensor_scan(st[0], e[0], e[0], T.BASE[:, 0:1], ALU.add, ALU.add),
            [st], [e, c("BASE", 0, 1)], vcost(st, e))
-        tt(c("M", 0, A), e, st, ALU.mult)
-        wrap("M", "D1")
-        ts(c("PL", 0, 24), c("D1", 0, 24), 1.0 / 8192, ALU.mult, float(H - 1), ALU.add)
+        tt(c("M", 0, A), c("E", 2, A + 2), c(SCAN, 2, A + 2), ALU.mult)
+        wrap("M", WRAP)
+        ts(c("PL", 0, 24), c(WRAP, 0, 24), 1.0 / 8192, ALU.mult, float(H - 1), ALU.add)
         cp(win("OW", A, "PL", 0, 24), c("NUM", 0, A))
-        wrap("OW", "D1")
-        ts(c("OL", 0, 24), c("D1", 0, 24), 1.0 / 65536, ALU.mult, float(H), ALU.add)
+        wrap("OW", WRAP)
+        ts(c("OL", 0, 24), c(WRAP, 0, 24), 1.0 / 65536, ALU.mult, float(H), ALU.add)
 
     def pick(src, lo, hi):
         return win(src, A, "OL", lo // 16, hi // 16)
 
-    def sort_s(lo, hi):
-        ts(c("SS", lo, hi), pick("SW", lo, hi), HOLE, ALU.min)
+    def holes(lo, hi):
+        act(c("TM", lo, hi), c("SS", lo, hi), AF.Relu, bias=BIG * HOLE, scale=-BIG)
 
-    def term_v(lo, hi):
-        act(c("TM", lo, hi), c("SS", lo, hi), bias=BIG * HOLE - 7 * HOLE, scale=-BIG)
-
-    def term_a(lo, hi):
-        act(c("TM", lo, hi), c("SS", lo, hi), bias=BIG * HOLE + HOLE, scale=-BIG)
-
-    def rob(lo, hi, bank, give_out):
-        ts(c("H2", lo, hi), c(bank, lo, hi), 0.5, ALU.is_le, HOLE, ALU.mult)
-        tt(c("H1", lo, hi), rev("SS", A - hi, A - lo), c(bank, lo, hi), ALU.max)
-        tt(give_out, rev("SS", A - hi, A - lo), c("H2", lo, hi), ALU.max)
-        tt(c("SS", lo, hi), c("SS", lo, hi), c("H1", lo, hi), ALU.min)
-
-    dma("a", at(T.UI[0:8, :], A, ("UI", 0, A)), hbm(T.u[:]), 1900)
-    k = dma("s", c("SRI", 0, A), hbm(T.sr[:]), 2600)
-    k = dma("s", c("LMI", 0, A), hbm(T.lim[:]), 3300, [(k, 0)])
-    dma("s", c("FIT", 0, W), hbm(T.fit[:]), 6000, [(k, 0)])
-    iota(c("PI", 0, 1), [[0, 1]], 0, 1, False)
-    iota(col(2), [[0, 1]], 0, 1, True)
-    iota(c("XG", 0, 128), [[1, 8], [0, 16]], 0, 0, True)
-    iota(c("XI", 0, 144), [[1, 144]], 0, 0, True)
-    iota(c("XT", 0, 4), [[1, 4]], 0, 0, True)
-    iota(c("NUM", 0, A), [[1, A]], -H, 0, True)
-    op("v", lambda: V.memset(T.CKD[:], -11 * HOLE), [c("CKD", 0, 128)], [], 70)
-    op("v", lambda: V.memset(T.CKA[:], -7 * HOLE), [c("CKA", 0, 64)], [], 70)
+    dma("a", [(rows("UI", 0, 8, 0, A), hbm(T.u[:]))], 1900)
+    k = dma("s", [(c("SRI", 0, A), hbm(T.sr[:]))], 2600)
+    k = dma("s", [(c("LMI", 0, A), hbm(T.lim[:]))], 3300, [(k, 0)])
+    dma("s", [(c("FIT", PAD, PAD + W), hbm(T.fit[:]))], 6000, [(k, 0)])
+    dma("s", [(c("FIT", PAD + W, PAD + 2 * W), c("FIT", PAD, PAD + W))], 5000)
+    iota(c("PI", 0, 1), [[0, 1]], 0, 1)
+    iota(col(2), [[0, 1]], 0, 1)
+    iota(c("XG", 0, 128), [[1, 8], [0, 16]], 0)
+    iota(c("XI", 0, 144), [[1, 144]], 0)
+    iota(c("XT", 0, 4), [[1, 4]], 0)
+    for j, bar in enumerate(BARS):
+        iota(c("CK", H * j, H * (j + 1)), [[0, H]], bar * 4096)
+    iota(c("NUM", 0, A), [[1, A]], -H)
+    iota(c("FIT", 0, PAD), [[0, PAD]], 256)
+    iota(msg("M1", RO - 1, 3), [[0, NB * BK]], 0)
     pi = c("PI", 0, 1)
     ts(c("PI", 1, 2), pi, 15, ALU.bitwise_and)
     ts(c("PI", 2, 3), pi, 4, ALU.arith_shift_right)
     ts(c("PI", 3, 4), pi, 1, ALU.arith_shift_right, 7, ALU.bitwise_and)
     ts(c("PI", 4, 5), pi, 1, ALU.bitwise_and)
-    r8 = at(T.R8[0:8, :], 128, ("R8", 0, 128))
-    ts(r8, at(T.XG[0:8, :], 128, ("XG", 0, 128)), at(T.COL[0:8, 2:3], 1, ("COL", 2, 3)), ALU.is_equal)
-    ts(col(0), c("PI", 1, 2), 2.0, ALU.mult, -16.0, ALU.add)
-    cp(col(3), c("PI", 2, 3))
-    ts(col(4), c("PI", 2, 3), 16.0, ALU.mult, 15.0, ALU.add)
-    cp(col(5), c("PI", 3, 4))
-    ts(col(7), c("PI", 4, 5), -63.0, ALU.mult, 64.0, ALU.add)
+    cp(c("COL", 16, 20), c("PI", 1, 5))
+    ci, cg, ct, cb = col(16), col(17), col(18), col(19)
+    r8 = rows("R8", 0, 8, 0, 128)
+    ts(r8, rows("XG", 0, 8, 0, 128), rows("COL", 0, 8, 2, 3), ALU.is_equal)
+    act(col(0), ci, scale=2.0, bias=-16.0)
+    act(col(1), ci, scale=2.0, bias=-17.0)
+    act(col(4), cg, scale=16.0, bias=15.0)
+    act(col(6), ct, scale=997.0)
+    act(col(7), cb, scale=-63.0, bias=64.0)
+    act(col(8), cb, scale=63.0, bias=1.0)
     ts(ID, c("XI", 0, 128), col(2), ALU.is_equal)
-    ts(BB, c("XG", 0, 128), col(3), ALU.is_equal)
+    ts(BB, c("XG", 0, 128), cg, ALU.is_equal)
     ts(c("Z", 0, 144), c("XI", 0, 144), col(4), ALU.is_equal, HOLE, ALU.mult)
-    act(col(1), col(0), bias=-1.0)
-    act(col(6), col(5), scale=997.0)
-    act(col(8), col(7), bias=65.0, scale=-1.0)
     act(NI, ID, scale=-1.0)
-    ts(c("COL", 12, 16), c("XT", 0, 4), col(5), ALU.is_equal, col(8), ALU.mult)
+    act(IB, ID, scale=16 * HOLE)
+    act(NB_, ID, scale=-16 * HOLE)
+    act(NH, ID, scale=-HOLE)
+    act(c("HV", 0, 128), ID, scale=-30 * HOLE)
+    act(c("HA", 0, 128), ID, scale=-28 * HOLE)
+    ts(c("COL", 12, 16), c("XT", 0, 4), ct, ALU.is_equal, col(8), ALU.mult)
     for t in range(RO):
         act(sv(t), BB, scale=col(12 + t))
 
-    uf = at(T.UF[0:8, :], A, ("UF", 0, A))
-    cp(uf, at(T.UI[0:8, :], A, ("UI", 0, A)))
+    uf = rows("UF", 0, 8, 0, A)
+    cp(uf, rows("UI", 0, 8, 0, A))
     mm(c("V", 0, A), r8, uf)
-    idx1(0, A, c("SRI", 0, A))
+    tt(c("PR", 0, A), c("SRI", 0, A), c("V", 0, A), ALU.mult)
     cp(c("LIM0", 0, A), c("LMI", 0, A))
-    idx2(0, A)
-    spread("LIM0", H, 256, act)
-    spread("LIM0", 0, H)
+    numbers(0, A)
+    cp(c("CU", 0, A), c("CX", 0, A))
+    for w in FIRSTWIDE:
+        spread("LIM0", *w)
     ts(c("KA", 0, A), c("V", 0, A), col(6), ALU.add, col(7), ALU.mult)
     ts(c("KB", 0, A), c("KA", 0, A), 6, ALU.arith_shift_right, 63, ALU.bitwise_and)
     cp(c("KV0", 0, A), c("KB", 0, A))
-    by_vector(0, 64, 0, "PA")
-    by_scalar(256, 320, "LIM0", "PB")
-    by_vector(64, 128, 0, "PA")
-    drop(0, 128, c("SRI", 0, 128), "PA")
-    by_scalar(320, A, "LIM0", "PB")
-    by_vector(128, H, 0, "PC")
-    drop(128, H, c("SRI", 128, H), "PC")
-    tally(0, H)
-    drop(256, A, c("SRI", 256, A), "PB")
-    tally(256, A)
-    by_vector(H, 256, H, "PA")
-    drop(H, 256, c("SRI", H, 256), "PA")
-    tally(H, 256)
+    for on, lo, hi in FIRST:
+        test(on, lo, hi, "LIM0", [w[:2] for w in FIRSTWIDE])
+    for lo, hi, bank in FIRSTSUM:
+        total(lo, hi, bank, (-11, -7))
+        tt(c("SW", lo, hi), c("SRI", lo, hi), c(bank, lo, hi), ALU.max)
+        tally(lo, hi)
+    classes(FIRSTSTAGES)
 
+    first = len(nodes)
     for t in range(RO - 1):
+        back[0] = len(nodes) - first
+        ring[:] = RING
         lo_, ln = "LIM%d" % (t % 2), "LIM%d" % ((t + 1) % 2)
         ko, kn = "KV%d" % (t % 2), "KV%d" % ((t + 1) % 2)
+        k2 = NB * BK * t
         mm(c("PA", 0, A), sv(t + 1), c(ko, 0, A))
         tt(c("KA", 0, A), c("SW", 0, A), c("PA", 0, A), ALU.mult)
         ts(c("KB", 0, A), c("KA", 0, A), 5, ALU.arith_shift_right, W - 1, ALU.bitwise_and)
+        mm(c("PB", 0, A), NH, c("HS", 0, A))
+        tt(c("KC", 0, A), c("KB", 0, A), c("PB", 0, A), ALU.add)
         order()
-        act(c(kn, 0, H), pick(ko, 0, H))
-        cp(c("CU", H, A), pick("KB", H, A))
-        sort_s(H, A)
-        sort_s(0, H)
+        both = max([H] + [hi for on, lo, hi in TESTS if on == "m"])
+        ts(c("CU", both, A), pick("KC", both, A), float(PAD), ALU.add)
+        for on, name, lo, hi in SORT:
+            new, old = {"K": (kn, ko), "S": ("SS", "SW"), "L": (ln, lo_)}[name]
+            (cp if on == "v" else act)(c(new, lo, hi), pick(old, lo, hi))
         mm(c("V", 0, H), sv(t), c(kn, 0, H))
-        act(c(ln, 0, H), pick(lo_, 0, H))
-        act(c(ln, H, ST), pick(lo_, H, ST))
-        act(c(kn, H, ST), pick(ko, H, ST))
-        idx1(0, H, rev("SS", H, A))
-        mm(c("V", 0, H), sv(t + 1), c(kn, 0, H))
-        idx2(0, H)
-        cp(m1all(t, 0), c("CU", ST, A))
-        for b in range(NB):
-            act(m1(t, b, 1), pick(lo_, ST + BK * b, ST + BK * (b + 1)))
-            act(m1(t, b, 2), pick(ko, ST + BK * b, ST + BK * (b + 1)))
+        mm(c("PC", H, A), sv(t + 1), c(kn, 0, H))
+        tt(c("PR", 0, H), rev("SS", H, A), c("V", 0, H), ALU.mult)
+        tt(c("PR", H, A), rev("SS", H, A), c("PC", H, A), ALU.mult)
+        numbers(0, H)
+        tt(c("CY", 0, H), pick("KC", 0, H), c("CX", 0, H), ALU.max)
+        ts(c("CU", 0, H), c("CY", 0, H), float(PAD), ALU.add)
+        numbers(H, A)
+        ts(c("CU", A, 2 * A - both), c("CX", H, H + A - both), float(PAD), ALU.add)
+        cp(msg("M1", t, 0), c("CU", ST, A))
+        copy(PACK[0], msg("M1", t, 1), c("SS", ST, A))
+        copy(PACK[1], msg("M1", t, 2), c(ln, ST, A))
+        copy(PACK[2], msg("M1", t, 3), c(kn, ST, A))
         send(1, t)
-        spread(ln, 0, 128)
-        term_v(0, 128)
-        term_a(128, H)
-        by_vector(0, 96, 0, "PA", c("TM", 0, 96))
-        by_scalar(128, H, ln, "PB", c("TM", 128, H))
-        rob(0, 96, "PA", rev("M2", 96 * t, 96 * (t + 1)))
-        send(2, t)
-        by_vector(96, 128, 0, "PB", c("TM", 96, 128))
-        by_scalar(H, 256, ln, "PC")
-        rob(96, H, "PB", rev("SS", H, ST))
-        give = len(nodes) - 2
-        idx1(0, 96, c("SS", 0, 96))
-        idx2(0, 96)
-        idx1(96, H, c("SS", 96, H))
-        nodes[-1]["after"].append((give, 0))
-        idx2(96, H)
-        by_scalar(128, H, ln, "PC")
-        by_vector(0, 64, 0, "PA")
-        by_vector(64, 128, 0, "PA")
-        cp(c("CU", ST, A), landed(t, 0))
-        act(c(ln, ST, A), landed(t, 1))
-        act(c(kn, ST, A), landed(t, 2))
-        spread4(ln, 320, A)
-        drop(128, 256, c("SS", 128, 256), "PC")
-        drop(0, 128, c("SS", 0, 128), "PA")
-        tally(0, 256)
-        by_scalar(256, 320, ln, "V")
-        by_vector(320, A, 320, "PB")
-        drop(256, ST, c("SS", 256, ST), "V")
-        drop(ST, 320, c("L2", 96 * t, 96 * t + 32), "V")
-        drop(320, A, c("L2", 96 * t + 32, 96 * (t + 1)), "PB")
-        tally(256, 320)
-        tally(320, A)
+        for w in WIDE:
+            if w[1] <= ST:
+                spread(ln, *w)
+        act(c("TM", 0, H), c("SS", 0, H), AF.Sign, bias=-(HOLE - 0.5))
+        wides = [w[:2] for w in WIDE]
+        todo = {"moves": list(MOVES), "sums": list(SUMS), "drops": list(DROPS), "tally": list(TALLY)}
+        done, moved, dropped = set(), set(), set()
+        landed = False
+        for on, lo, hi in TESTS:
+            if lo < A and hi > ST and not landed:
+                landed = True
+                cp(c("CU", ST, A), msg("L1", t, 0))
+                copy(PACK[3], c(ln, ST, A), msg("L1", t, 2))
+                copy(PACK[4], c(kn, ST, A), msg("L1", t, 3))
+                for w in WIDE:
+                    if w[1] > ST:
+                        spread(msg("L1", t, 2, (w[0] - ST) // BK, (w[1] - ST) // BK) if w[3][0] == "g" else ln, *w)
+            if on == "m":
+                assert moved >= set(range(A - hi, A - lo))
+                tt(c("KA", lo, hi), pick("KC", lo, hi), c("MV", H * t + lo - H, H * t + hi - H), ALU.mult)
+                tt(c("KA", lo, hi), c("KA", lo, hi), rev("CX", H + A - hi, H + A - lo), ALU.max)
+                ts(c("CU", lo, hi), c("KA", lo, hi), float(PAD), ALU.add)
+                done |= set(range(A + lo, A + hi))
+            test(on, lo, hi, ln, wides, (0, PAD + 2 * W))
+            done |= set(range(lo, hi))
+            for p, q, bank in list(todo["moves"]):
+                if done >= set(range(p, q)):
+                    todo["moves"].remove((p, q, bank))
+                    total(p, q, bank, (-41, -35), [(a, b, c("H" + shape[a][0].upper(), 0, 128), c("TM", a, b))
+                                                   for a, b in alike(p, q)])
+                    act(rev("MV", H * t + H - q, H * t + H - p), c(bank, p, q), AF.Sign, bias=63.5 * HOLE)
+                    if p < A - ST and moved | set(range(p, q)) >= set(range(A - ST)):
+                        send(2, t)
+                    tt(c("SW", p, q), c("SS", p, q), c(bank, p, q), ALU.max)
+                    moved |= set(range(p, q))
+            for p, q, b2 in list(todo["sums"]):
+                if p >= A - both and done >= set(range(2 * A - q, 2 * A - p)):
+                    todo["sums"].remove((p, q, b2))
+                    lo, hi = A - q, A - p
+                    total(A + lo, A + hi, b2, (5, 9), last=[(lo, hi, IB, c("MV", H * t + lo - H, H * t + hi - H))])
+                    tt(c(b2, lo - H, hi - H), c("SS", lo, hi), c(b2, lo, hi), ALU.max)
+                    tt(c("SW", p, q), c("SW", p, q), rev(b2, lo - H, hi - H), ALU.min)
+                elif p < A - both and done >= set(range(A + p, A + q)) and moved >= set(range(p, q)):
+                    todo["sums"].remove((p, q, b2))
+                    total(A + p, A + q, b2, (5, 9), last=[(p, q, IB, rev("MV", H * t + H - q, H * t + H - p))])
+                    tt(c(b2, H + p, H + q), rev("SS", A - q, A - p), c(b2, p, q), ALU.max)
+                    tt(c("SW", p, q), c("SW", p, q), c(b2, H + p, H + q), ALU.min)
+            for p, q, bank in list(todo["drops"]):
+                if done >= set(range(p, q)) and moved >= set(range(A - min(q, ST), A - p)):
+                    todo["drops"].remove((p, q, bank))
+                    last = []
+                    if p < ST:
+                        last.append((p, min(q, ST), NB_, c("MV", H * t + p - H, H * t + min(q, ST) - H)))
+                    if q > ST:
+                        last.append((max(p, ST), q, NB_, c("L2", k2 + max(p, ST) - ST, k2 + q - ST)))
+                    total(p, q, bank, (5, 9), last=last)
+                    if not any(a <= p < b for a, b in TALLY):
+                        tally(p, q, bank)
+                    if p < ST:
+                        tt(c("SW", p, min(q, ST)), c("SS", p, min(q, ST)), c(bank, p, min(q, ST)), ALU.max)
+                    if q > ST:
+                        a = max(p, ST)
+                        tt(c("SW", a, q), msg("L1", t, 1, (a - ST) // BK, (q - ST) // BK), c(bank, a, q), ALU.max)
+                    dropped |= set(range(p, q))
+        assert not (todo["moves"] or todo["sums"] or todo["drops"])
+        for p, q in TALLY:
+            tally(p, q)
+        classes(STAGES)
 
     t = RO - 1
+    back[0] = 0
     lo_, ln, ko, kn = "LIM1", "LIM0", "KV1", "KV0"
-    order()
-    act(c(kn, 0, 96), pick(ko, 0, 96))
-    sort_s(ST, A)
-    mm(c("V", 0, 96), sv(t), c(kn, 0, 96))
-    act(c(ln, 0, 96), pick(lo_, 0, 96))
-    sort_s(0, 96)
-    idx1(0, 96, rev("SS", ST, A))
-    idx2(0, 96)
-    act(c(kn, 96, ST), pick(ko, 96, ST))
-    mm(c("V", 96, H), sv(t), c(kn, 96, H))
-    spread4(ln, 0, 64)
-    term_v(0, 64)
-    term_a(64, 96)
-    for b in range(NB):
-        act(m1(t, b, 1), pick(lo_, ST + BK * b, ST + BK * (b + 1)))
-        act(m1(t, b, 2), pick(ko, ST + BK * b, ST + BK * (b + 1)))
-    send(1, t)
-    by_vector(0, 32, 0, "PA", c("TM", 0, 32))
-    by_scalar(64, 96, ln, "PC", c("TM", 64, 96))
-    by_vector(32, 64, 0, "PB", c("TM", 32, 64))
-    rob(0, 32, "PA", rev("M2", 96 * t + 64, 96 * t + 96))
-    rob(64, 96, "PC", rev("M2", 96 * t, 96 * t + 32))
-    rob(32, 64, "PB", rev("M2", 96 * t + 32, 96 * t + 64))
-    send(2, t)
-    sort_s(96, ST)
-    act(c(ln, 96, ST), pick(lo_, 96, ST))
-    idx1(96, H, rev("SS", H, ST))
-    idx2(96, H)
-    spread4(ln, 96, 160)
-    term_v(96, 160)
-    term_a(160, H)
-    by_scalar(160, H, ln, "PA", c("TM", 160, H), "D1")
-    by_vector(96, 160, 96, "PA", c("TM", 96, 160))
-    rob(96, H, "PA", rev("SS", H, ST))
-    act(c("OUTL", 0, ST), c(ln, 0, ST))
-    dma("s", hbm(T.ylim[:, 0:ST]), c("OUTL", 0, ST), 2400)
-    dma("s", hbm(T.ysr[:, 0:ST]), c("SS", 0, ST), 2400)
-    act(c(kn, ST, A), landed(t, 2))
-    v8 = at(T.V[0:8, 0:A], A, ("V", 0, A))
-    mm(v8, c("SV", 0, 128, 16), c(kn, 0, A))
-    k8 = at(T.OUTK[0:8, :], A, ("OUTK", 0, A))
-    act(k8, v8)
-    dma("s", hbm(T.ylim[:, ST:A]), landed(t, 1), 2000)
-    dma("a", hbm(T.yu[:]), k8, 1900)
-    dma("s", hbm(T.ysr[:, ST:A]), c("L2", 96 * t, 96 * (t + 1)), 2000)
 
-    ends = emit(g, T, arrange(nodes))
-    for name in ends:
-        g.wait_ge(T.sem[name], ends[name])
-    g.wait_ge(T.sem.sent, sent[0])
+    def lists(lo, hi, bank):
+        mm(c(bank, lo, hi), sv(t), c(kn, lo, hi))
+        tt(c("PR", lo, hi), rev("SS", A - hi, A - lo), c(bank, lo, hi), ALU.mult)
+        numbers(lo, hi)
+        cp(c("CU", lo, hi), c("CX", lo, hi))
+
+    def rob(lo, hi, bank):
+        total(lo, hi, bank, (-7, 1), [(lo, hi, ID, c("TM", lo, hi))])
+        give = rev("SS", A - hi, A - lo)
+        ts(c(bank, H + lo, H + hi), c(bank, lo, hi), 0.5, ALU.is_le, HOLE, ALU.mult)
+        tt(rev("SW", A - hi, A - lo), give, c(bank, H + lo, H + hi), ALU.max)
+        tt(c(bank, lo, hi), give, c(bank, lo, hi), ALU.max)
+        tt(c("SW", lo, hi), c("SS", lo, hi), c(bank, lo, hi), ALU.min)
+
+    ts(c("SW", 0, A), c("SW", 0, A), HOLE, ALU.min)
+    ring[:] = ["D0", "D1", "H2"]
+    order()
+    for on, name, lo, hi in LSORT:
+        new, old = {"K": (kn, ko), "S": ("SS", "SW"), "L": (ln, lo_), "O": ("OUTL", lo_)}[name]
+        copy(on, c(new, lo, hi), pick(old, lo, hi))
+    lists(0, A - ST, "V")
+    lists(A - ST, H, "PB")
+    wides = [w[:2] for w in LASTW]
+    for w in LASTW:
+        spread(ln, *w)
+    holes(0, A - ST)
+    holes(A - ST, H)
+    copy(LPACK, msg("M1", t, 2), c("OUTL", ST, A))
+    k = NB * t
+    mm(rows("H1", 0, 8, 0, A), c("SV", 0, 128, 16), c(kn, 0, A))
+    act(at(T.M1[0:8, k:k + NB, 3 * BK:4 * BK], NB * BK, *msg("M1", t, 3)[3:]), rows("H1", 0, 8, ST, A))
+    send(1, t)
+    for on, lo, hi in LAST:
+        test(on, lo, hi, ln, wides)
+    for lo, hi, bank in LASTSUM:
+        rob(lo, hi, bank)
+    send(2, t)
+    act(rows("OUTK", 0, 8, 0, ST), rows("H1", 0, 8, 0, ST))
+    dma("s", [(hbm(T.ylim[:, 0:ST]), c("OUTL", 0, ST))], 2400)
+    dma("s", [(hbm(T.yu[:, 0:ST]), rows("OUTK", 0, 8, 0, ST))], 1900)
+    dma("s", [(hbm(T.ylim[:, ST:A]), msg("L1", t, 2)),
+              (hbm(T.yu[:, ST:A]), at(T.L1[0:8, k:k + NB, 3 * BK:4 * BK], NB * BK, *msg("L1", t, 3)[3:]))], 2000)
+    dma("s", [(hbm(T.ysr[:, 0:ST]), c("SW", 0, ST))], 2400)
+    dma("a", [(hbm(T.ysr[:, ST:A]), c("L3", 0, NB * BK))], 2000)
+    return nodes, sent[0]

from concourse.bass import DstId, RemoteDMATransfer
from concourse.mybir import AluOpType, ActivationFunctionType

ALU = AluOpType
AF = ActivationFunctionType
A, H, ST, BK, NB, RO, W = 384, 192, 288, 32, 3, 4, 4096
HOLE = 4096.0
BIG = 131072.0
CFG = {"gam": 1.3, "sig": 3.2, "cyc": 0.83, "pe": 0.42, "hop": 160, "vfix": 20, "afix": 60, "riss": 700, "rlat": 1100,
       "late": 300, "tries": 16000, "moves": 2, "tied": 0.9, "seed": 3, "aim": 0, "heat": 300.0,
       "polish": 2000, "far": 4, "warm": 50.0}
CASES = [(1.0, 1.0, 0.0), (0.8, 1.0, 1500.0), (1.33, 1.5, 0.0)]
FIRST = [("v", 0, 64), ("a", 192, 256), ("v", 64, 128), ("a", 256, 320), ("v", 128, 192), ("v", 320, 384)]
FIRSTSUM = [(0, 128, "PA"), (192, 256, "PB"), (128, 192, "PC"), (256, 320, "V"), (320, 384, "PA")]
FIRSTWIDE = [(0, 128, 16, "v"), (128, 192, 16, "a"), (320, 384, 4, "gg")]
LASTW = [(0, 32, 4, "vv"), (64, 96, 4, "aa"), (96, 128, 4, "gg")]
LAST = [("v", 0, 32), ("v", 64, 96), ("a", 32, 64), ("a", 128, 192), ("v", 96, 128)]
LASTSUM = [(0, 32, "PA"), (64, 96, "PC"), (32, 64, "PB"), (96, 192, "V")]
LSORT = [("a", "K", 0, 96), ("v", "S", 288, 384), ("a", "L", 0, 96), ("a", "K", 96, 192), ("v", "S", 192, 288),
         ("v", "S", 0, 96), ("a", "L", 96, 192), ("a", "S", 96, 192), ("a", "K", 192, 384), ("a", "O", 288, 384),
         ("a", "O", 0, 288)]
LPACK = "g"
PACK = "ggggg"
SORT = [("a", "K", 0, 192), ("v", "S", 192, 384), ("a", "L", 0, 192), ("a", "S", 0, 192), ("a", "L", 192, 384),
        ("a", "K", 192, 384)]
WIDE = [(0, 128, 16, "v"), (320, 384, 4, "gv")]
TESTS = [("a", 192, 256), ("v", 0, 96), ("a", 128, 192), ("v", 96, 128), ("v", 384, 448), ("a", 512, 576),
         ("v", 448, 512), ("a", 256, 320), ("v", 320, 352), ("v", 352, 384)]
RING = ["D0", "D1", "H1", "H2"]
MOVES = [(0, 96, "PA"), (96, 192, "V")]
SUMS = [(0, 64, "PB"), (128, 192, "PC"), (64, 128, "PB")]
DROPS = [(192, 256, "PB"), (256, 320, "V"), (320, 384, "PA")]
TALLY = [(0, 128), (128, 256)]
STAGES = [(0, 256, "D0", "D1"), (256, 384, "PC", "PB")]
FIRSTSTAGES = [(0, 256, "H1", "H2"), (256, 384, "PC", "PB")]
SCAN, WRAP = "H1", "H2"
PAD = 16
PLAN = {}


def sb(n, dtype):
    return ("sbuf", [128, n], dtype)


SCRATCH = {
    "FIT": sb(PAD + 2 * W, "bfloat16"), "SRI": sb(A, "int32"), "LMI": sb(A, "int32"), "UI": sb(A, "int32"), "UF": sb(A, "float32"),
    "XI": sb(144, "float32"), "XG": sb(128, "float32"), "XT": sb(4, "float32"), "PI": sb(8, "int32"),
    "COL": sb(24, "float32"), "NUM": sb(A, "bfloat16"), "ID": sb(128, "bfloat16"), "NI": sb(128, "bfloat16"),
    "HV": sb(128, "bfloat16"), "HA": sb(128, "bfloat16"), "IB": sb(128, "bfloat16"), "NH": sb(128, "bfloat16"), "NB": sb(128, "bfloat16"),
    "Z": sb(144, "bfloat16"), "BB": sb(128, "bfloat16"), "SV": sb(512, "bfloat16"), "R8": sb(128, "float32"),
    "CK": sb(7 * H, "bfloat16"), "SW": sb(A, "float32"), "SS": sb(A, "float32"),
    "LIM0": sb(A, "bfloat16"), "LIM1": sb(A, "bfloat16"), "KV0": sb(A, "bfloat16"), "KV1": sb(A, "bfloat16"),
    "PR": sb(A, "int32"), "CX": sb(A, "int32"), "CY": sb(H, "int32"), "CU": sb(A + H, "uint16"),
    "KA": sb(A, "int32"), "KB": sb(A, "int32"), "KC": sb(A, "int32"),
    "LX": sb(16 * A, "bfloat16"), "L4": sb(8 * A, "bfloat16"),
    "IND": sb(16 * (A + ST), "bfloat16"), "REC": sb(16 * (A + H), "bfloat16"),
    "HS": sb(A, "bfloat16"), "JK": sb(A, "bfloat16"), "E": sb(A + 2, "bfloat16"), "M": sb(A, "bfloat16"),
    "OW": sb(A, "bfloat16"), "BASE": sb(4, "float32"), "PL": sb(24, "uint16"), "OL": sb(24, "uint16"),
    "TM": sb(H, "bfloat16"), "MV": sb(RO * H, "bfloat16"),
    "M1": ("sbuf", [128, RO * NB, 4 * BK], "float32"), "L1": ("sbuf", [128, RO * NB, 4 * BK], "float32"),
    "L2": sb(RO * NB * BK, "bfloat16"), "L3": sb(NB * BK, "float32"),
    "OUTL": sb(A, "float32"), "OUTK": sb(A, "float32"),
}
for bank_ in ("D0", "D1", "PA", "PB", "PC", "V", "H1", "H2"):
    SCRATCH[bank_] = ("psum", [128, 512], "float32")
NDMA = 12
SEMAPHORES = (["q_v", "q_a", "q_p", "q_g", "sent"] + ["dm%d" % k for k in range(NDMA)]
              + ["a%d_%d" % (kd, t) for kd in (1, 2) for t in range(RO)])
BARS = [-11, -7, -41, -35, 5, 9, 1]


def routes(T, topo):
    n = len(T.cores)
    out = {}
    for r, src in enumerate(T.cores):
        used = []
        for b in range(NB):
            dst = T.cores[(r + 1 + b) % n]
            via = None
            if not topo.may_write(src, dst):
                can = [c for c in topo.cores_of(src)
                       if c not in T.cores and c not in used and topo.may_write(c, dst)]
                can.sort(key=lambda c: topo.die(c) != topo.die(src))
                via = can[0]
                used.append(via)
            out[(r, b)] = (dst, via)
    return out


def bits(engines):
    m = 0
    for e in engines:
        m |= 1 << e
    return m


def relay_masks(T, topo, rt, r):
    src = T.cores[r]
    bl = [b for b in range(NB) if rt[(r, b)][1] is not None]
    out = {}
    for j, b in enumerate(bl):
        eng = topo.engines(src, rt[(r, b)][1])
        n = len(eng) // len(bl)
        out[b] = eng[j * n:(j + 1) * n]
    return out


def place_of(kind, land, t, b):
    k = NB * t + b
    if kind == 1:
        return ("L1" if land else "M1", k, k + 1)
    if t < RO - 1:
        return ("L2", BK * k, BK * (k + 1)) if land else ("MV", H * t + ST - H + BK * b, H * t + ST - H + BK * (b + 1))
    return ("L3", BK * b, BK * (b + 1)) if land else ("SW", ST + BK * b, ST + BK * (b + 1))


def piece(T, kind, land, t, b):
    name, lo, hi = place_of(kind, land, t, b)
    if kind == 1:
        return T[name][:, lo, (2 * BK if t == RO - 1 else 0):4 * BK]
    return T[name][:, lo:hi]


def relay_program(g, core, T, topo, rt):
    total = 0
    for (r, b) in [k for k in rt if rt[k][1] == core]:
        dst = rt[(r, b)][0]
        n_in = len(relay_masks(T, topo, rt, r)[b])
        rid, pid = topo.addr(dst, core)
        for t in range(RO):
            for kind in (1, 2):
                sem = T.sem["a%d_%d" % (kind, t)]
                g.wait_ge(sem, n_in)
                ap = piece(T, kind, True, t, b)
                g.remote_dma(ap, ap, sem, T.sem.sent, pid, rid, topo.mask(core, dst))
                total += len(topo.engines(core, dst))
    if total:
        g.wait_ge(T.sem.sent, total)


def clash(x, y, qx, qy):
    if SCRATCH[x[0]][0] == "psum":
        if qx == "p" and qy == "p":
            return False
        if qx != qy:
            return True
    return (x[3] or y[3]) and x[1] < y[2] and y[1] < x[2]


def depends(nodes):
    pred = [dict() for _ in nodes]
    by_buf = {}
    for k, nd in enumerate(nodes):
        acc = set(x for o in nd["ops"] for x in o["acc"])
        for x in acc:
            for (j, y) in by_buf.get(x[0], []):
                if j in pred[k]:
                    continue
                if nd["q"] == "p" and nodes[j]["q"] == "p":
                    if SCRATCH[x[0]][0] == "psum":
                        pred[k][j] = 0
                elif clash(x, y, nd["q"], nodes[j]["q"]):
                    pred[k][j] = nodes[j]["lat"] + CFG["hop"]
        for j, d in nd["after"]:
            pred[k][j] = max(pred[k].get(j, 0), d)
        for x in acc:
            by_buf.setdefault(x[0], []).append((k, x))
    far = [set() for _ in nodes]
    for k in range(len(nodes)):
        for j in sorted(pred[k], reverse=True):
            if j in far[k] and nodes[j]["lat"] == 0 and pred[k][j] <= CFG["hop"] and nodes[j]["q"] is not None:
                del pred[k][j]
            else:
                far[k] |= far[j]
                far[k].add(j)
    return pred


def arrange(nodes):
    n = len(nodes)
    if n in PLAN:
        return [o for k in PLAN[n] for o in nodes[k]["ops"]]
    pred = depends(nodes)
    pl = [list(p.items()) for p in pred]
    sl = [[] for _ in nodes]
    for k in range(n):
        for j, d in pl[k]:
            sl[j].append((k, d))
    busy = [nd["busy"] for nd in nodes]
    qs = [nd["q"] for nd in nodes]
    tail = [nd["lat"] for nd in nodes]
    cases = []
    for gather, other, late in CASES:
        cases.append([x * (gather if nd["ops"][0]["ind"] else other) + (late if nd["q"] is None else 0.0)
                      for x, nd in zip(busy, nodes)])

    def place(extra):
        level = [0.0] * n
        for k in range(n - 1, -1, -1):
            top = tail[k]
            for s, d in sl[k]:
                if d + level[s] > top:
                    top = d + level[s]
            level[k] = busy[k] + extra[k] + 0.001 + top
        taken = {}
        start, end = [0.0] * n, [0.0] * n
        for k in sorted(range(n), key=lambda j: -level[j]):
            st = 0.0
            for j, d in pl[k]:
                if end[j] + d > st:
                    st = end[j] + d
            if qs[k]:
                spans = taken.setdefault(qs[k], [])
                i = len(spans)
                while i and spans[i - 1][1] > st:
                    i -= 1
                while i < len(spans) and st + busy[k] > spans[i][0]:
                    st = max(st, spans[i][1])
                    i += 1
                spans.insert(i, (st, st + busy[k]))
            else:
                st += CFG["late"]
            start[k], end[k] = st, st + busy[k]
        return sorted(range(n), key=lambda j: (start[j], j))

    def length(seq):
        total = 0.0
        for bz in cases:
            end = [0.0] * n
            free = {}
            top = 0.0
            for k in seq:
                st = free.get(qs[k], 0.0) if qs[k] else 0.0
                for j, d in pl[k]:
                    if end[j] + d > st:
                        st = end[j] + d
                end[k] = free[qs[k]] = st + bz[k]
                if end[k] + tail[k] > top:
                    top = end[k] + tail[k]
            total += top
        return total

    def held(seq, bz):
        end, why = [0.0] * n, [None] * n
        last = {}
        for k in seq:
            j0 = last.get(qs[k]) if qs[k] else None
            st = 0.0
            for j, d in pl[k]:
                if end[j] + d > st:
                    st, why[k] = end[j] + d, (j, False)
            if j0 is not None and end[j0] > st:
                st, why[k] = end[j0], (j0, True)
            end[k] = st + bz[k]
            last[qs[k]] = k
        k = max(range(n), key=lambda j: end[j] + tail[j])
        out = []
        while why[k]:
            if why[k][1]:
                out.append((why[k][0], k))
            k = why[k][0]
        return out

    twins = {}
    for k, nd in enumerate(nodes):
        twins.setdefault(nd["twin"], []).append(k)
    extra = [0.0] * n
    seq = place(extra)
    best = length(seq)
    pairs = [p for bz in cases for p in held(seq, bz)]
    seed = [CFG["seed"]]

    def draw(m):
        seed[0] = (seed[0] * 1103515245 + 12345) % 2147483648
        return (seed[0] >> 8) % m

    for step in range(CFG["tries"]):
        other = list(extra)
        aim = draw(100) < CFG["aim"]
        mid = pairs[draw(len(pairs))] if aim else [draw(n)] * 2
        for move in range(CFG["moves"]):
            if aim and move == 0:
                up = draw(2)
                k = mid[up]
                to = extra[k] + draw(800) if up else max(-busy[k], extra[k] - draw(800))
            else:
                k = min(n - 1, max(0, mid[0] + draw(40) - 20))
                to = draw(1000) * 1.5 if draw(3) else 0.0
            for j in (twins[nodes[k]["twin"]] if step < CFG["tied"] * CFG["tries"] else [k]):
                other[j] = to
            if aim and draw(2):
                break
        s2 = place(other)
        now = length(s2)
        if now <= best + CFG["heat"] * (1.0 - step / CFG["tries"]) * draw(100) / 100.0:
            best, extra, seq = now, other, s2
            pairs = [p for bz in cases for p in held(seq, bz)]

    up, down = [0] * n, [0] * n
    for k in range(n):
        for j, d in pl[k]:
            up[k] |= up[j] | 1 << j
    for k in range(n - 1, -1, -1):
        for j, d in sl[k]:
            down[k] |= down[j] | 1 << j

    def shift(seq, j, k, early):
        a, b = seq.index(j), seq.index(k)
        if a > b or up[k] >> j & 1:
            return seq
        span = seq[a:b + 1]
        mask = up[k] | 1 << k if early else ~(down[j] | 1 << j)
        return seq[:a] + [x for x in span if mask >> x & 1] + [x for x in span if not mask >> x & 1] + seq[b + 1:]

    keep = (best, seq)
    for step in range(CFG["polish"]):
        j, k = pairs[draw(len(pairs))]
        back, early = draw(CFG["far"]), draw(2)
        if early:
            ahead = [x for x in seq[:seq.index(j) + 1] if qs[x] == qs[k]]
            j = ahead[max(0, len(ahead) - 1 - back)]
        else:
            behind = [x for x in seq[seq.index(k):] if qs[x] == qs[k]]
            k = behind[min(len(behind) - 1, back)]
        s2 = seq
        tj, tk = twins[nodes[j]["twin"]], twins[nodes[k]["twin"]]
        for x, y in (zip(tj, tk) if len(tj) == len(tk) and tj.index(j) == tk.index(k) else [(j, k)]):
            s2 = shift(s2, x, y, early)
        now = length(s2)
        if now <= best + CFG["warm"] * (1.0 - step / CFG["polish"]) * draw(100) / 100.0:
            best, seq = now, s2
            pairs = [p for bz in cases for p in held(seq, bz)]
            if best < keep[0]:
                keep = (best, seq)
    seq = keep[1]
    PLAN[n] = seq
    return [o for k in seq for o in nodes[k]["ops"]]


def emit(g, T, ops):
    eng = {"v": g.vector, "a": g.scalar, "p": g.tensor, "g": g, "s": g.sync}
    known = {q: {} for q in eng}
    seq = {q: 0 for q in eng}
    by_buf = {}
    for k, op in enumerate(ops):
        q = op["q"]
        if q is not None and op.get("sem") is None:
            seq[q] += 1
            op["line"], op["pos"] = q, seq[q]
        else:
            op["line"], op["pos"] = "x%d" % k, 1
        op["waits"] = []
        op["marked"] = False
        op["knows"] = {}
        if q is not None:
            need = {}
            for x in op["acc"]:
                for (j, y) in by_buf.get(x[0], []):
                    o = ops[j]
                    oq = o["line"]
                    if known[q].get(oq, 0) < o["pos"] and clash(x, y, op["line"], oq) and need.get(oq, (0, 0))[0] < o["pos"]:
                        need[oq] = (o["pos"], j)
            for (pos, j) in sorted(need.values(), key=lambda z: -z[1]):
                o = ops[j]
                if known[q].get(o["line"], 0) >= o["pos"]:
                    continue
                op["waits"].append(j)
                o["marked"] = True
                for ln, p in o["knows"].items():
                    if known[q].get(ln, 0) < p:
                        known[q][ln] = p
            op["knows"] = dict(known[q])
        op["knows"][op["line"]] = op["pos"]
        for x in op["acc"]:
            by_buf.setdefault(x[0], []).append((k, x))
    count = {q: 0 for q in eng}
    ends = {}
    waited = {}
    for op in ops:
        q = op["q"]
        for j in op["waits"]:
            eng[q].wait_ge(T.sem[ops[j]["sem"]], ops[j]["val"])
            waited[ops[j]["sem"]] = max(waited.get(ops[j]["sem"], 0), ops[j]["val"])
        if q is None:
            ends[op["sem"]] = op["val"]
            continue
        ins = op["fn"]()
        if op.get("remote"):
            continue
        if op.get("sem") is not None:
            for i in ins:
                i.then_inc(T.sem[op["sem"]], 16)
            ends[op["sem"]] = op["val"]
        elif op["marked"]:
            count[q] += 1
            op["sem"], op["val"] = "q_" + q, count[q]
            ins.then_inc(T.sem[op["sem"]], 1)
            ends[op["sem"]] = count[q]
    return {name: ends[name] for name in ends if waited.get(name, 0) < ends[name]}


def rank_program(g, core, T, topo):
    rt = routes(T, topo)
    if T.rank_of(core) is None:
        relay_program(g, core, T, topo, rt)
        return
    nodes, sent = calls(g, core, T, topo, rt)
    ends = emit(g, T, arrange(nodes))
    for name in ends:
        g.wait_ge(T.sem[name], ends[name])
    g.wait_ge(T.sem.sent, sent)


def calls(g, core, T, topo, rt):
    rank = T.rank_of(core)
    nodes = []
    ndma = [0]
    sent = [0]
    back = [0]
    V, S, P = g.vector, g.scalar, g.tensor
    cyc = CFG["cyc"]

    def at(ap, n, *regions):
        return (ap, n, (SCRATCH[regions[0][0]][0], SCRATCH[regions[0][0]][2] in ("bfloat16", "uint16"))) + regions

    def c(name, lo, hi, step=1):
        ap = T[name][:, lo:hi:step] if step != 1 else T[name][:, lo:hi]
        return at(ap, len(range(lo, hi, step)), (name, lo, hi))

    def rows(name, p0, p1, lo, hi):
        return at(T[name][p0:p1, lo:hi], hi - lo, (name, lo, hi))

    def rev(name, lo, hi):
        return at(T[name][:, hi - 1:lo - 1:-1] if lo > 0 else T[name][:, hi - 1::-1], hi - lo, (name, lo, hi))

    def win(name, n, off, lo, hi):
        a, b = n if isinstance(n, tuple) else (0, n)
        return (T[name][:, a:b].indirect(T[off][:, lo:hi]), 16 * (hi - lo), "win", (name, a, b), (off, lo, hi))

    def op(q, fn, outs, ins, busy, lat=0.0, join=False, after=(), **kw):
        acc = []
        for o in outs:
            if o[2] == "win":
                acc += [o[3] + (True,), o[4] + (False,)]
            else:
                acc += [r + (True,) for r in o[3:]]
        for i in ins:
            if isinstance(i, tuple):
                acc += [r + (False,) for r in i[3:]]
        d = {"q": q, "fn": fn, "acc": acc,
             "ind": any(isinstance(x, tuple) and x[2] == "win" for x in list(outs) + list(ins))}
        d.update(kw)
        if join:
            nodes[-1]["ops"].append(d)
            nodes[-1]["busy"] += busy
        else:
            nodes.append({"q": q, "ops": [d], "busy": busy, "lat": lat, "after": list(after),
                          "twin": len(nodes) - back[0]})
        return len(nodes) - 1

    def val(x):
        return x[0] if isinstance(x, tuple) else x

    def vcost(out, in0, per=None):
        if out[2] == "win":
            return 50 + out[1] * CFG["sig"]
        if in0[2] == "win":
            return 50 + out[1] * CFG["gam"]
        if per is None:
            per = 0.5 if out[2][1] and in0[2][1] else 1.0
        return CFG["vfix"] + max(64, out[1] * per) * cyc

    def ts(out, in0, s1, op0, s2=None, op1=None):
        if op1 is None:
            op("v", lambda: V.tensor_scalar(out[0], in0[0], val(s1), None, op0), [out], [in0, s1], vcost(out, in0))
        else:
            op("v", lambda: V.tensor_scalar(out[0], in0[0], val(s1), val(s2), op0, op1), [out], [in0, s1, s2], vcost(out, in0))

    def tt(out, in0, in1, o):
        per = 2.0 if in0[2][0] == "sbuf" and in1[2][0] == "sbuf" else 1.0
        op("v", lambda: V.tensor_tensor(out[0], in0[0], in1[0], o), [out], [in0, in1], vcost(out, in0, per))

    def cp(out, in_):
        op("v", lambda: V.tensor_copy(out[0], in_[0]), [out], [in_], vcost(out, in_))

    def act(out, in_, func=AF.Identity, bias=0.0, scale=1.0, accum=None):
        busy = 65 + out[1] * CFG["gam"] if in_[2] == "win" else CFG["afix"] + out[1] * cyc
        if accum is None:
            op("a", lambda: S.activation(out[0], in_[0], func, bias=val(bias), scale=val(scale)),
               [out], [in_, bias, scale], busy)
        else:
            op("a", lambda: S.activation(out[0], in_[0], func, bias=val(bias), scale=val(scale), accum_out=accum[0]),
               [out, accum], [in_, bias, scale], busy)

    def mm(out, lhsT, rhs, start=True, stop=True, join=False):
        op("p", lambda: P.matmul(out[0], lhsT[0], rhs[0], start, stop), [out], [lhsT, rhs],
           max(64, rhs[1]) * CFG["pe"] * (1 if rhs[2][1] else 4), join=join)

    def dma(q, pairs, lat, after=()):
        e = g.sync if q == "s" else g.scalar
        name = "dm%d" % ndma[0]
        ndma[0] += 1
        return op(q, lambda: [e.dma_start(o[0], i[0]) for o, i in pairs], [o for o, i in pairs], [i for o, i in pairs],
                  60 * len(pairs), lat, after=after, sem=name, val=16 * len(pairs))

    def hbm(ap):
        return (ap, 0, "hbm")

    def iota(out, pattern, base, cm=0):
        busy = 130 + 2 * out[1] * cyc
        if SCRATCH[out[3][0]][2] != "int32":
            op("g", lambda: g.iota(out[0], pattern, base, cm, allow_small_or_imprecise_dtypes=True), [out], [], busy)
        else:
            op("g", lambda: g.iota(out[0], pattern, base, cm), [out], [], busy)

    def col(k):
        return c("COL", k, k + 1)

    rm = relay_masks(T, topo, rt, rank)
    chain = []

    def send(kd, t):
        name = "a%d_%d" % (kd, t)
        sem = T.sem[name]
        trs = []
        edges = []
        for b in rm:
            rid, pid = topo.addr(rt[(rank, b)][1], core)
            trs.append(RemoteDMATransfer(dst_ids=[DstId(rid=rid, pnc=pid)], dma_engine_mask=bits(rm[b]), remote_sem=sem,
                                         src=piece(T, kd, False, t, b), dst=piece(T, kd, True, t, b)))
            sent[0] += len(rm[b])
        if trs:
            k = op("g", lambda: g.remote_dma_fused(trs, local_sem=T.sem.sent), [],
                   [at(None, 0, place_of(kd, False, t, b)) for b in rm], CFG["riss"], after=chain[-1:], remote=True,
                   relayed=(kd, t))
            chain.append((k, 0))
            edges.append((k, 2 * CFG["rlat"] + CFG["riss"] + 2 * CFG["hop"]))
        for b in range(NB):
            if b in rm:
                continue
            dst = rt[(rank, b)][0]
            rid, pid = topo.addr(dst, core)
            sent[0] += len(topo.engines(core, dst))
            k = op("g", lambda b=b, dst=dst, rid=rid, pid=pid: g.remote_dma(
                piece(T, kd, True, t, b), piece(T, kd, False, t, b), sem, T.sem.sent, pid, rid,
                topo.mask(core, dst)), [], [at(None, 0, place_of(kd, False, t, b))], CFG["riss"], remote=True)
            edges.append((k, CFG["rlat"]))
        n = 0
        for (r, b), (dst, via) in rt.items():
            if dst == core:
                n += len(topo.engines(via if via is not None else T.cores[r], core))
        op(None, None, [at(None, 0, place_of(kd, True, t, b)) for b in range(NB)], [], 0, after=edges, sem=name, val=n)

    def msg(name, t, part, b0=0, b1=NB):
        k = NB * t
        return at(T[name][:, k + b0:k + b1, part * BK:(part + 1) * BK], (b1 - b0) * BK,
                  *[(name, k + b + part / 4.0, k + b + (part + 1) / 4.0) for b in range(b0, b1)])

    ID, NI, IB, NB_, NH, BB = [c(n, 0, 128) for n in ("ID", "NI", "IB", "NB", "NH", "BB")]

    def sel(r):
        return c("Z", 15 - r, 143 - r)

    def sv(t):
        return c("SV", 128 * t, 128 * (t + 1))

    def copy(on, out, in_):
        if on == "g":
            op("g", lambda: g.affine_select(out[0], in_[0], [[0, out[1]]], ALU.is_ge, 0.0, 0, 0), [out], [in_],
               170 + 2 * out[1] * cyc)
        else:
            (cp if on == "v" else act)(out, in_)

    def spread(src, lo, hi, k, on):
        mid, m = ("LX" if k == 16 else "L4"), 16 // k
        for j in range(k):
            copy(on[0], at(T[mid][:, k * lo + j:k * hi:k], hi - lo, (mid, k * lo + j / 32.0, k * lo + (j + 1) / 32.0)),
                 c(src, lo, hi) if isinstance(src, str) else src)
        for j in range(m if m > 1 else 0):
            copy(on[1 + j % (len(on) - 1)],
                 at(T.LX[:, 16 * lo + j:16 * hi:m], k * (hi - lo), ("LX", 16 * lo + j / 32.0, 16 * lo + (j + 1) / 32.0)),
                 at(T.L4[:, k * lo:k * hi], k * (hi - lo), ("L4", k * lo, k * lo + 1)))

    def numbers(lo, hi):
        ts(c("CX", lo, hi), c("PR", lo, hi), 5, ALU.arith_shift_right, W - 1, ALU.bitwise_and)

    shape = {}

    ring = ["D0", "D1"]

    def test(on, lo, hi, lim, wides, span=(PAD, PAD + W)):
        n, a = hi - lo, lo % A
        for j in range(lo, hi):
            shape[j] = (on, lo, hi)
        if on == "v":
            part = max(p for p, q in wides if p <= a)
            tt(c("IND", 16 * lo, 16 * hi), win("FIT", span, "CU", lo, hi),
               at(T.LX[:, 16 * a:16 * (a + n)], 16 * n, ("LX", 16 * part, 16 * part + 1)), ALU.is_gt)
            return
        act(c("REC", 16 * lo, 16 * hi), win("FIT", span, "CU", lo, hi))
        sides = [(lo, c(lim, a, a + n))]
        if on == "m":
            sides.insert(0, (A + lo, rev(lim, A - hi, A - lo)))
        for to, limits in sides:
            banks = [ring.pop(0) for _ in range(2 if n > 32 else 1)]
            ring.extend(banks)
            for j in range(to, to + n):
                shape[j] = ("a", to, to + n)
            k = 16 // len(banks)
            for h, d in enumerate(banks):
                for i in range(k):
                    mm(c(d, i * n, (i + 1) * n), NI, limits, i == 0, False, join=i > 0)
                for i in range(k):
                    mm(c(d, i * n, (i + 1) * n), ID, c("REC", 16 * lo + h * k + i, 16 * hi, 16), False, i == k - 1,
                       join=i > 0)
                act(c("IND", 16 * to + h * k * n, 16 * to + (h + 1) * k * n), c(d, 0, k * n), AF.Sign, bias=-0.5)

    def alike(lo, hi):
        cuts = [lo] + [j for j in range(lo + 1, hi) if shape[j] != shape[j - 1] and "a" in (shape[j][0], shape[j - 1][0])] + [hi]
        return list(zip(cuts, cuts[1:]))

    def total(lo, hi, bank, bar, first=(), last=()):
        cuts = alike(lo, hi)
        for j, (p, q) in enumerate(cuts):
            k = H * BARS.index(bar[shape[p][0] == "a"])
            mm(c(bank, p % A, p % A + q - p), ID, c("CK", k, k + q - p), j == 0, False, join=j > 0)
        for a, b, st, mv in first:
            mm(c(bank, a, b), st, mv, False, False)
        for j, (p, q) in enumerate(cuts):
            on, l0, h0 = shape[p]
            for i in range(16):
                src = c("IND", 16 * p + i, 16 * q, 16) if on == "v" else \
                    c("IND", 16 * l0 + i * (h0 - l0) + p - l0, 16 * l0 + i * (h0 - l0) + q - l0)
                mm(c(bank, p % A, p % A + q - p), sel(i), src, False,
                   i == 15 and j == len(cuts) - 1 and not last,
                   join=i % (16 if on == "v" else 8) > 0)
        for j, (a, b, st, mv) in enumerate(last):
            mm(c(bank, a, b), st, mv, False, j == len(last) - 1)

    def tally(lo, hi, src="SW"):
        act(c("HS", lo, hi), c(src, lo, hi), AF.Sign, bias=-(HOLE - 0.5))

    def classes(stages):
        for j, (lo, hi, b1, b2) in enumerate(stages):
            mm(c(b2, lo, hi), BB, c("HS", lo, hi))
            mm(c(b1, lo, hi), BB, c("HS", lo, hi))
            ts(c("E", 2 + lo, 2 + hi), c(b1, lo, hi), 14.0, ALU.min, col(0), ALU.is_equal)
            act(c("JK", lo, hi), c(b2, lo, hi), AF.Sign, bias=col(1), scale=-1.0, accum=c("BASE", 1 - j, 2 - j))
            if j == 0:
                act(c("E", 1, 2), c("BASE", 1, 2), scale=0.5)

    def wrap(src, bank):
        for r in range(16):
            mm(c(bank, 0, 24), sel(r), c(src, r, A, 16), r == 0, r == 15, join=r != 0)

    def order():
        e, st = c("E", 1, A + 2), c(SCAN, 1, A + 2)
        op("v", lambda: V.tensor_tensor_scan(st[0], e[0], e[0], T.BASE[:, 0:1], ALU.add, ALU.add),
           [st], [e, c("BASE", 0, 1)], vcost(st, e))
        tt(c("M", 0, A), c("E", 2, A + 2), c(SCAN, 2, A + 2), ALU.mult)
        wrap("M", WRAP)
        ts(c("PL", 0, 24), c(WRAP, 0, 24), 1.0 / 8192, ALU.mult, float(H - 1), ALU.add)
        cp(win("OW", A, "PL", 0, 24), c("NUM", 0, A))
        wrap("OW", WRAP)
        ts(c("OL", 0, 24), c(WRAP, 0, 24), 1.0 / 65536, ALU.mult, float(H), ALU.add)

    def pick(src, lo, hi):
        return win(src, A, "OL", lo // 16, hi // 16)

    def holes(lo, hi):
        act(c("TM", lo, hi), c("SS", lo, hi), AF.Relu, bias=BIG * HOLE, scale=-BIG)

    dma("a", [(rows("UI", 0, 8, 0, A), hbm(T.u[:]))], 1900)
    k = dma("s", [(c("SRI", 0, A), hbm(T.sr[:]))], 2600)
    k = dma("s", [(c("LMI", 0, A), hbm(T.lim[:]))], 3300, [(k, 0)])
    dma("s", [(c("FIT", PAD, PAD + W), hbm(T.fit[:]))], 6000, [(k, 0)])
    dma("s", [(c("FIT", PAD + W, PAD + 2 * W), c("FIT", PAD, PAD + W))], 5000)
    iota(c("PI", 0, 1), [[0, 1]], 0, 1)
    iota(col(2), [[0, 1]], 0, 1)
    iota(c("XG", 0, 128), [[1, 8], [0, 16]], 0)
    iota(c("XI", 0, 144), [[1, 144]], 0)
    iota(c("XT", 0, 4), [[1, 4]], 0)
    for j, bar in enumerate(BARS):
        iota(c("CK", H * j, H * (j + 1)), [[0, H]], bar * 4096)
    iota(c("NUM", 0, A), [[1, A]], -H)
    iota(c("FIT", 0, PAD), [[0, PAD]], 256)
    iota(msg("M1", RO - 1, 3), [[0, NB * BK]], 0)
    pi = c("PI", 0, 1)
    ts(c("PI", 1, 2), pi, 15, ALU.bitwise_and)
    ts(c("PI", 2, 3), pi, 4, ALU.arith_shift_right)
    ts(c("PI", 3, 4), pi, 1, ALU.arith_shift_right, 7, ALU.bitwise_and)
    ts(c("PI", 4, 5), pi, 1, ALU.bitwise_and)
    cp(c("COL", 16, 20), c("PI", 1, 5))
    ci, cg, ct, cb = col(16), col(17), col(18), col(19)
    r8 = rows("R8", 0, 8, 0, 128)
    ts(r8, rows("XG", 0, 8, 0, 128), rows("COL", 0, 8, 2, 3), ALU.is_equal)
    act(col(0), ci, scale=2.0, bias=-16.0)
    act(col(1), ci, scale=2.0, bias=-17.0)
    act(col(4), cg, scale=16.0, bias=15.0)
    act(col(6), ct, scale=997.0)
    act(col(7), cb, scale=-63.0, bias=64.0)
    act(col(8), cb, scale=63.0, bias=1.0)
    ts(ID, c("XI", 0, 128), col(2), ALU.is_equal)
    ts(BB, c("XG", 0, 128), cg, ALU.is_equal)
    ts(c("Z", 0, 144), c("XI", 0, 144), col(4), ALU.is_equal, HOLE, ALU.mult)
    act(NI, ID, scale=-1.0)
    act(IB, ID, scale=16 * HOLE)
    act(NB_, ID, scale=-16 * HOLE)
    act(NH, ID, scale=-HOLE)
    act(c("HV", 0, 128), ID, scale=-30 * HOLE)
    act(c("HA", 0, 128), ID, scale=-28 * HOLE)
    ts(c("COL", 12, 16), c("XT", 0, 4), ct, ALU.is_equal, col(8), ALU.mult)
    for t in range(RO):
        act(sv(t), BB, scale=col(12 + t))

    uf = rows("UF", 0, 8, 0, A)
    cp(uf, rows("UI", 0, 8, 0, A))
    mm(c("V", 0, A), r8, uf)
    tt(c("PR", 0, A), c("SRI", 0, A), c("V", 0, A), ALU.mult)
    cp(c("LIM0", 0, A), c("LMI", 0, A))
    numbers(0, A)
    cp(c("CU", 0, A), c("CX", 0, A))
    for w in FIRSTWIDE:
        spread("LIM0", *w)
    ts(c("KA", 0, A), c("V", 0, A), col(6), ALU.add, col(7), ALU.mult)
    ts(c("KB", 0, A), c("KA", 0, A), 6, ALU.arith_shift_right, 63, ALU.bitwise_and)
    cp(c("KV0", 0, A), c("KB", 0, A))
    for on, lo, hi in FIRST:
        test(on, lo, hi, "LIM0", [w[:2] for w in FIRSTWIDE])
    for lo, hi, bank in FIRSTSUM:
        total(lo, hi, bank, (-11, -7))
        tt(c("SW", lo, hi), c("SRI", lo, hi), c(bank, lo, hi), ALU.max)
        tally(lo, hi)
    classes(FIRSTSTAGES)

    first = len(nodes)
    for t in range(RO - 1):
        back[0] = len(nodes) - first
        ring[:] = RING
        lo_, ln = "LIM%d" % (t % 2), "LIM%d" % ((t + 1) % 2)
        ko, kn = "KV%d" % (t % 2), "KV%d" % ((t + 1) % 2)
        k2 = NB * BK * t
        mm(c("PA", 0, A), sv(t + 1), c(ko, 0, A))
        tt(c("KA", 0, A), c("SW", 0, A), c("PA", 0, A), ALU.mult)
        ts(c("KB", 0, A), c("KA", 0, A), 5, ALU.arith_shift_right, W - 1, ALU.bitwise_and)
        mm(c("PB", 0, A), NH, c("HS", 0, A))
        tt(c("KC", 0, A), c("KB", 0, A), c("PB", 0, A), ALU.add)
        order()
        both = max([H] + [hi for on, lo, hi in TESTS if on == "m"])
        ts(c("CU", both, A), pick("KC", both, A), float(PAD), ALU.add)
        for on, name, lo, hi in SORT:
            new, old = {"K": (kn, ko), "S": ("SS", "SW"), "L": (ln, lo_)}[name]
            (cp if on == "v" else act)(c(new, lo, hi), pick(old, lo, hi))
        mm(c("V", 0, H), sv(t), c(kn, 0, H))
        mm(c("PC", H, A), sv(t + 1), c(kn, 0, H))
        tt(c("PR", 0, H), rev("SS", H, A), c("V", 0, H), ALU.mult)
        tt(c("PR", H, A), rev("SS", H, A), c("PC", H, A), ALU.mult)
        numbers(0, H)
        tt(c("CY", 0, H), pick("KC", 0, H), c("CX", 0, H), ALU.max)
        ts(c("CU", 0, H), c("CY", 0, H), float(PAD), ALU.add)
        numbers(H, A)
        ts(c("CU", A, 2 * A - both), c("CX", H, H + A - both), float(PAD), ALU.add)
        cp(msg("M1", t, 0), c("CU", ST, A))
        copy(PACK[0], msg("M1", t, 1), c("SS", ST, A))
        copy(PACK[1], msg("M1", t, 2), c(ln, ST, A))
        copy(PACK[2], msg("M1", t, 3), c(kn, ST, A))
        send(1, t)
        for w in WIDE:
            if w[1] <= ST:
                spread(ln, *w)
        act(c("TM", 0, H), c("SS", 0, H), AF.Sign, bias=-(HOLE - 0.5))
        wides = [w[:2] for w in WIDE]
        todo = {"moves": list(MOVES), "sums": list(SUMS), "drops": list(DROPS), "tally": list(TALLY)}
        done, moved, dropped = set(), set(), set()
        landed = False
        for on, lo, hi in TESTS:
            if lo < A and hi > ST and not landed:
                landed = True
                cp(c("CU", ST, A), msg("L1", t, 0))
                copy(PACK[3], c(ln, ST, A), msg("L1", t, 2))
                copy(PACK[4], c(kn, ST, A), msg("L1", t, 3))
                for w in WIDE:
                    if w[1] > ST:
                        spread(msg("L1", t, 2, (w[0] - ST) // BK, (w[1] - ST) // BK) if w[3][0] == "g" else ln, *w)
            if on == "m":
                assert moved >= set(range(A - hi, A - lo))
                tt(c("KA", lo, hi), pick("KC", lo, hi), c("MV", H * t + lo - H, H * t + hi - H), ALU.mult)
                tt(c("KA", lo, hi), c("KA", lo, hi), rev("CX", H + A - hi, H + A - lo), ALU.max)
                ts(c("CU", lo, hi), c("KA", lo, hi), float(PAD), ALU.add)
                done |= set(range(A + lo, A + hi))
            test(on, lo, hi, ln, wides, (0, PAD + 2 * W))
            done |= set(range(lo, hi))
            for p, q, bank in list(todo["moves"]):
                if done >= set(range(p, q)):
                    todo["moves"].remove((p, q, bank))
                    total(p, q, bank, (-41, -35), [(a, b, c("H" + shape[a][0].upper(), 0, 128), c("TM", a, b))
                                                   for a, b in alike(p, q)])
                    act(rev("MV", H * t + H - q, H * t + H - p), c(bank, p, q), AF.Sign, bias=63.5 * HOLE)
                    if p < A - ST and moved | set(range(p, q)) >= set(range(A - ST)):
                        send(2, t)
                    tt(c("SW", p, q), c("SS", p, q), c(bank, p, q), ALU.max)
                    moved |= set(range(p, q))
            for p, q, b2 in list(todo["sums"]):
                if p >= A - both and done >= set(range(2 * A - q, 2 * A - p)):
                    todo["sums"].remove((p, q, b2))
                    lo, hi = A - q, A - p
                    total(A + lo, A + hi, b2, (5, 9), last=[(lo, hi, IB, c("MV", H * t + lo - H, H * t + hi - H))])
                    tt(c(b2, lo - H, hi - H), c("SS", lo, hi), c(b2, lo, hi), ALU.max)
                    tt(c("SW", p, q), c("SW", p, q), rev(b2, lo - H, hi - H), ALU.min)
                elif p < A - both and done >= set(range(A + p, A + q)) and moved >= set(range(p, q)):
                    todo["sums"].remove((p, q, b2))
                    total(A + p, A + q, b2, (5, 9), last=[(p, q, IB, rev("MV", H * t + H - q, H * t + H - p))])
                    tt(c(b2, H + p, H + q), rev("SS", A - q, A - p), c(b2, p, q), ALU.max)
                    tt(c("SW", p, q), c("SW", p, q), c(b2, H + p, H + q), ALU.min)
            for p, q, bank in list(todo["drops"]):
                if done >= set(range(p, q)) and moved >= set(range(A - min(q, ST), A - p)):
                    todo["drops"].remove((p, q, bank))
                    last = []
                    if p < ST:
                        last.append((p, min(q, ST), NB_, c("MV", H * t + p - H, H * t + min(q, ST) - H)))
                    if q > ST:
                        last.append((max(p, ST), q, NB_, c("L2", k2 + max(p, ST) - ST, k2 + q - ST)))
                    total(p, q, bank, (5, 9), last=last)
                    if not any(a <= p < b for a, b in TALLY):
                        tally(p, q, bank)
                    if p < ST:
                        tt(c("SW", p, min(q, ST)), c("SS", p, min(q, ST)), c(bank, p, min(q, ST)), ALU.max)
                    if q > ST:
                        a = max(p, ST)
                        tt(c("SW", a, q), msg("L1", t, 1, (a - ST) // BK, (q - ST) // BK), c(bank, a, q), ALU.max)
                    dropped |= set(range(p, q))
        assert not (todo["moves"] or todo["sums"] or todo["drops"])
        for p, q in TALLY:
            tally(p, q)
        classes(STAGES)

    t = RO - 1
    back[0] = 0
    lo_, ln, ko, kn = "LIM1", "LIM0", "KV1", "KV0"

    def lists(lo, hi, bank):
        mm(c(bank, lo, hi), sv(t), c(kn, lo, hi))
        tt(c("PR", lo, hi), rev("SS", A - hi, A - lo), c(bank, lo, hi), ALU.mult)
        numbers(lo, hi)
        cp(c("CU", lo, hi), c("CX", lo, hi))

    def rob(lo, hi, bank):
        total(lo, hi, bank, (-7, 1), [(lo, hi, ID, c("TM", lo, hi))])
        give = rev("SS", A - hi, A - lo)
        ts(c(bank, H + lo, H + hi), c(bank, lo, hi), 0.5, ALU.is_le, HOLE, ALU.mult)
        tt(rev("SW", A - hi, A - lo), give, c(bank, H + lo, H + hi), ALU.max)
        tt(c(bank, lo, hi), give, c(bank, lo, hi), ALU.max)
        tt(c("SW", lo, hi), c("SS", lo, hi), c(bank, lo, hi), ALU.min)

    ts(c("SW", 0, A), c("SW", 0, A), HOLE, ALU.min)
    ring[:] = ["D0", "D1", "H2"]
    order()
    for on, name, lo, hi in LSORT:
        new, old = {"K": (kn, ko), "S": ("SS", "SW"), "L": (ln, lo_), "O": ("OUTL", lo_)}[name]
        copy(on, c(new, lo, hi), pick(old, lo, hi))
    lists(0, A - ST, "V")
    lists(A - ST, H, "PB")
    wides = [w[:2] for w in LASTW]
    for w in LASTW:
        spread(ln, *w)
    holes(0, A - ST)
    holes(A - ST, H)
    copy(LPACK, msg("M1", t, 2), c("OUTL", ST, A))
    k = NB * t
    mm(rows("H1", 0, 8, 0, A), c("SV", 0, 128, 16), c(kn, 0, A))
    act(at(T.M1[0:8, k:k + NB, 3 * BK:4 * BK], NB * BK, *msg("M1", t, 3)[3:]), rows("H1", 0, 8, ST, A))
    send(1, t)
    for on, lo, hi in LAST:
        test(on, lo, hi, ln, wides)
    for lo, hi, bank in LASTSUM:
        rob(lo, hi, bank)
    send(2, t)
    act(rows("OUTK", 0, 8, 0, ST), rows("H1", 0, 8, 0, ST))
    dma("s", [(hbm(T.ylim[:, 0:ST]), c("OUTL", 0, ST))], 2400)
    dma("s", [(hbm(T.yu[:, 0:ST]), rows("OUTK", 0, 8, 0, ST))], 1900)
    dma("s", [(hbm(T.ylim[:, ST:A]), msg("L1", t, 2)),
              (hbm(T.yu[:, ST:A]), at(T.L1[0:8, k:k + NB, 3 * BK:4 * BK], NB * BK, *msg("L1", t, 3)[3:]))], 2000)
    dma("s", [(hbm(T.ysr[:, 0:ST]), c("SW", 0, ST))], 2400)
    dma("a", [(hbm(T.ysr[:, ST:A]), c("L3", 0, NB * BK))], 2000)
    return nodes, sent[0]
